import numpy as np
import ml_dtypes


def mxq(x, axis, fmt="e4m3"):
    dtype, down = {"e4m3": (ml_dtypes.float8_e4m3fn, 7), "e5m2": (ml_dtypes.float8_e5m2, 14)}[fmt]
    v = np.moveaxis(np.asarray(x, np.float32).astype(ml_dtypes.bfloat16).astype(np.float64), axis, -1)
    blocks = v.reshape(v.shape[:-1] + (-1, 32))
    amax = np.abs(blocks).max(-1, keepdims=True)
    byte = np.maximum(np.where(amax > 0, np.frexp(amax)[1] - 1 + 127, 0) - down, 1)
    scale = np.exp2(byte - 127.0)
    codes = (blocks / scale).astype(np.float32).astype(dtype).astype(np.float64)
    return np.moveaxis((codes * scale).reshape(v.shape), -1, axis)


WIDE = False


def mx_kscale(k):
    if not WIDE:
        return np.ones(k)
    levels = np.array([10, -10, 5, -5, 0])
    if k % 512:
        return np.exp2(np.random.permutation(np.resize(levels, k // 32))).repeat(32)
    a = np.empty((k // 512, 16))
    for p in range(k // 512):
        a[p, :8] = np.random.permutation(np.resize(levels, 8))
        for g in range(8):
            far = levels[np.abs(levels - a[p, g]) >= 10]
            a[p, g + 8] = far[np.random.randint(len(far))]
    return np.exp2(a.ravel()).repeat(32)


def f64(x):
    return np.asarray(x).astype(np.float64)


def striped(idx):
    return np.tile(idx.reshape(-1, 16).T, (8, 1)).astype(np.uint16)


def unstriped(offs):
    return offs[:16].T.reshape(-1).astype(np.int64)


E2M1 = np.array([0.0, 0.5, 1.0, 1.5, 2.0, 3.0, 4.0, 6.0, -0.0, -0.5, -1.0, -1.5, -2.0, -3.0, -4.0, -6.0])


def pack_weight(w, fmt):
    k, n = w.shape
    w = f64(np.asarray(w, np.float32).astype(ml_dtypes.bfloat16)).reshape(k // 32, 32, n)
    amax = np.abs(w).max(1)
    if fmt == "e4m3":
        byte = np.frexp(amax)[1] - 1 + 127 - 7
    else:
        mant, ex = np.frexp(amax / 6.0)
        byte = np.where(mant > 0.5, ex, ex - 1) + 127
    byte = np.clip(np.where(amax > 0, byte, 1), 1, 254)
    scaled = (w * np.exp2(127.0 - byte)[:, None, :]).reshape(k, n).astype(np.float32)
    by_word = np.ascontiguousarray(scaled.reshape(k // 512, 128, 4, n).transpose(0, 1, 3, 2))
    if fmt == "e4m3":
        words = by_word.astype(ml_dtypes.float8_e4m3fn).view(np.uint8)
    else:
        c = by_word.astype(ml_dtypes.float4_e2m1fn).view(np.uint8) & 0xF
        words = (c[..., 0::2] | (c[..., 1::2] << 4)).reshape(k // 512, 128, 2 * n)
    return np.ascontiguousarray(words), np.ascontiguousarray(byte.astype(np.uint8).reshape(k // 512, 16, n))


def unpack_weight(words, scales, fmt):
    g, _, n = scales.shape
    words = np.ascontiguousarray(words).reshape(g, 128, n, -1)
    if fmt == "e4m3":
        vals = words.view(ml_dtypes.float8_e4m3fn).astype(np.float64)
    else:
        nib = np.empty((g, 128, n, 4), np.uint8)
        nib[..., 0::2] = words & 0xF
        nib[..., 1::2] = words >> 4
        vals = E2M1[nib]
    vals = vals * np.repeat(np.exp2(scales.astype(np.float64) - 127.0), 8, axis=1)[..., None]
    return vals.transpose(0, 1, 3, 2).reshape(g * 512, n)


def gelu(v):
    return 0.5 * v * (1.0 + np.tanh(np.sqrt(2.0 / np.pi) * (v + 0.044715 * v**3)))


K, T, S, H, T2, P = 1024, 2048, 512, 1024, 1024, 512

def setup_inputs():
    n = np.random.standard_normal
    s = mx_kscale(K)[:, None]
    u = mx_kscale(H)[:, None]
    d = {}
    d["tab_words"], d["tab_scales"] = pack_weight(n((K, T)) * s, "e4m3")
    d["offs"] = striped(np.random.permutation(T)[:S])
    d["offs2"] = striped(np.random.permutation(T2)[:S])
    d["offs3"] = striped(np.random.permutation(T2)[:P])
    d["w1"] = (0.48 * n((K, H)) / K**0.5 / s * u.T).astype(np.float32)
    d["w2_words"], d["w2_scales"] = pack_weight(n((K, H)) / K**0.5 / s, "e2m1")
    d["w3_words"], d["w3_scales"] = pack_weight(0.64 * n((K, H)) / K**0.5 / s * u.T, "e4m3")
    d["wgs"] = np.exp(0.3 * n((128, S))).astype(np.float32)
    d["page0"] = (n((H, T2)) * u).astype(np.float32)
    d["low"] = (0.5 * n(H) * u[:, 0]).astype(np.float32)
    sign = np.random.choice([-1.0, 1.0], H)
    d["look"] = (0.42 * sign * np.random.uniform(0.6, 1.4, H) / u[:, 0]**2 / H**0.5).astype(np.float32)
    d["slot"] = (np.random.choice([-1.0, 1.0], T2) * np.random.uniform(0.3, 1.0, T2)).astype(np.float32)
    return d

def reference(tab_words, tab_scales, offs, offs2, offs3, w1, w2_words, w2_scales, w3_words, w3_scales, wgs, page0, low, look, slot):
    v = unpack_weight(tab_words, tab_scales, "e4m3")[:, unstriped(offs)]
    a = mxq(f64(w1), 0, "e4m3").T @ v
    b = unpack_weight(w2_words, w2_scales, "e2m1").T @ v
    c = unpack_weight(w3_words, w3_scales, "e4m3").T @ v
    h = a * np.abs(b) - c
    page = f64(page0).copy()
    page[:, unstriped(offs2)] = np.tile(f64(wgs), (H // 128, 1)) * h
    x = np.maximum(page[:, unstriped(offs3)], f64(low)[:, None]) * f64(look)[:, None]
    e = mxq(page, 0, "e4m3").T @ mxq(x, 0, "e4m3")
    return np.cos(e + f64(slot)[:, None])

@@ -1,0 +1,304 @@
+import math
+from contextlib import ExitStack
+
+import concourse.mybir as mybir
+from concourse.masks import make_identity
+
+K, T, S, H, T2, NX = 1024, 2048, 512, 1024, 1024, 512
+FLOPS = 2 * K * H * S * 3 + 2 * H * T2 * NX
+
+F32 = mybir.dt.float32
+BF16 = mybir.dt.bfloat16
+I32 = mybir.dt.int32
+U32 = mybir.dt.uint32
+U16 = mybir.dt.uint16
+U8 = mybir.dt.uint8
+FP8X4 = mybir.dt.float8_e4m3fn_x4
+FP4X4 = mybir.dt.float4_e2m1fn_x4
+ALU = mybir.AluOpType
+ACT = mybir.ActivationFunctionType
+
+P = 128
+PACK = 4
+PASS = P * PACK
+W3_ROW = 4
+W1_VECTOR_COLS = 336
+X_VECTOR_COLS = 192
+ABS_TILES = 3
+
+
+def weave(engine_copy, dst, src, c0, c1):
+    engine_copy(
+        out=dst[:, c0:c1, :].rearrange("p (c i) t -> p c t i", i=4),
+        in_=src[:, :, c0:c1].rearrange("p t (c i) -> p c t i", i=4),
+    )
+
+
+def tile_list_mix_slot_readout_kernel(
+    tc, tab_words, tab_scales, offs, offs2, offs3, w1, w2_words, w2_scales, w3_words, w3_scales,
+    wgs, page0, low, look, slot, out,
+):
+    nc = tc.nc
+    with ExitStack() as ctx:
+        lists = ctx.enter_context(tc.tile_pool(name="lists", bufs=1))
+        sb = ctx.enter_context(tc.tile_pool(name="sb", bufs=1))
+        ps = ctx.enter_context(tc.psum_pool(name="ps", bufs=2))
+
+        def new_tile(shape, dtype, name, tag=None, bufs=1):
+            return sb.tile(shape, dtype, name=name, tag=tag or name, bufs=bufs, align_bytes=64)
+
+        idx = lists.tile([P, S // 16], U16, name="idx")
+        idx2 = lists.tile([P, S // 16], U16, name="idx2")
+        idx3 = lists.tile([P, NX // 16], U16, name="idx3")
+
+        tab_w = [new_tile([P, T], I32, "tab_w%d" % a) for a in range(2)]
+        wg = []
+        tab_s = new_tile([P, 2, T], U8, "tab_s")
+        w2_s = new_tile([P, 2, H], U8, "w2_s")
+        w3_s = new_tile([P, 2, H], U8, "w3_s")
+        w2_w = [new_tile([P, 2, 2 * PASS], U8, "w2_w%d" % b) for b in range(2)]
+        w3_w = [new_tile([P, 2, PASS], U32, "w3_w%d" % b) for b in range(2)]
+        page = [[new_tile([P, T2], F32, "page%d%d" % (b, t)) for t in range(PACK)] for b in range(2)]
+        low_t = new_tile([P, 2, PACK], F32, "low_t")
+        look_t = new_tile([P, 2, PACK], F32, "look_t")
+        slot_t = new_tile([P, T2 // P], F32, "slot_t")
+        half_slot = new_tile([P, T2 // P], F32, "half_slot")
+        ident = new_tile([P, P], F32, "ident")
+
+        def load_table_words(a):
+            nc.sync.dma_start(tab_w[a][:], tab_words[a].rearrange("p n i -> p (n i)").bitcast(I32))
+
+        def load_scales(queue, plane, row0, scales):
+            for q in range(4):
+                queue.dma_start(
+                    plane[32 * q + row0 : 32 * q + row0 + 4].bitcast(I32),
+                    scales[:, 4 * q : 4 * q + 4, :].rearrange("a r n -> r a n").bitcast(I32),
+                )
+
+        def load_w1(a, b):
+            raw = new_tile([P, PACK, PASS], F32, "w1_raw%d%d" % (a, b), tag="raw", bufs=2)
+            rows = w1[a * PASS : (a + 1) * PASS, b * PASS : (b + 1) * PASS]
+            nc.sync.dma_start(raw[:], rows.rearrange("(p i) c -> p i c", i=PACK))
+            return raw
+
+        def load_w23(b):
+            nc.sync.dma_start(
+                w2_w[b][:].bitcast(I32),
+                w2_words[:, :, 2 * b * PASS : 2 * (b + 1) * PASS].rearrange("a p n -> p a n").bitcast(I32),
+            )
+            nc.sync.dma_start(
+                w3_w[b][:].bitcast(I32),
+                w3_words[:, :, b * PASS : (b + 1) * PASS, :].rearrange("a p n i -> p a (n i)").bitcast(I32),
+            )
+
+        def load_wg(queue, t0, tag):
+            wg.append(new_tile([P, 2, S], F32, "wg%d" % t0, tag))
+            for q in range(4):
+                queue.dma_start(
+                    wg[-1][32 * q : 32 * q + 32],
+                    wgs.rearrange("(p t) j -> p t j", t=PACK)[:, t0 : t0 + 2, :],
+                )
+
+        def load_page(b, t):
+            rows = page0[b * PASS : (b + 1) * PASS, :].rearrange("(p t) m -> p t m", t=PACK)
+            nc.sync.dma_start(page[b][t][:], rows[:, t, :])
+
+        def quantize(grouped, width, name):
+            codes = new_tile([P, width], U32, name + "_c")
+            scales = new_tile([P, width], U8, name + "_s")
+            nc.vector.quantize_mx(
+                out=codes[:].bitcast(FP8X4), scales=scales[:], in_=grouped[:].rearrange("p c t -> p (c t)")
+            )
+            return codes, scales
+
+        def quantize_w1(raw, a, b, vector_cols, slot_of=("w1_bf", 2)):
+            grouped = new_tile([P, PASS, PACK], BF16, "w1_bf%d%d" % (a, b), *slot_of)
+            if vector_cols:
+                weave(nc.vector.tensor_copy, grouped, raw, 0, vector_cols)
+            step = P if vector_cols == 0 else PASS - vector_cols
+            for c0 in range(vector_cols, PASS, step):
+                weave(nc.scalar.copy, grouped, raw, c0, c0 + step)
+            return quantize(grouped, PASS, "w1_%d%d" % (a, b))
+
+        nc.vector.memset(tab_s[:].bitcast(I32), 0)
+        nc.gpsimd.memset(w2_s[:].bitcast(I32), 0)
+        nc.vector.memset(w3_s[:].bitcast(I32), 0)
+        nc.sync.dma_start(idx[:], offs)
+        load_table_words(0)
+        load_scales(nc.sync, tab_s, 0, tab_scales)
+        raw00 = load_w1(0, 0)
+        load_table_words(1)
+        raw10 = load_w1(1, 0)
+        load_w23(0)
+        load_scales(nc.gpsimd, w2_s, 0, w2_scales)
+        load_scales(nc.gpsimd, w3_s, W3_ROW, w3_scales)
+        make_identity(nc, ident[:])
+        nc.sync.dma_start(idx2[:], offs2)
+        load_page(0, 0)
+        load_page(0, 1)
+        load_wg(nc.sync, 0, "wg0")
+        nc.gpsimd.dma_start(low_t[:], low.rearrange("(b p t) -> p b t", b=2, t=PACK))
+        nc.gpsimd.dma_start(look_t[:], look.rearrange("(b p t) -> p b t", b=2, t=PACK))
+
+        v_w, v_s = [], []
+        w1_q = {}
+        for a, raw in ((0, raw00), (1, raw10)):
+            words = new_tile([P, S], U32, "v_w%d" % a)
+            nc.vector.tensor_copy(words[:], tab_w[a][:].bitcast(U32).indirect(idx[:]))
+            planes = new_tile([P, S], U8, "v_s%d" % a)
+            nc.vector.tensor_copy(planes[:], tab_s[:, a, :].indirect(idx[:]))
+            v_w.append(words)
+            v_s.append(planes)
+            w1_q[a, 0] = quantize_w1(raw, a, 0, W1_VECTOR_COLS)
+
+        raw01 = load_w1(0, 1)
+        load_page(0, 2)
+        raw11 = load_w1(1, 1)
+        load_w23(1)
+        load_page(0, 3)
+        nc.sync.dma_start(idx3[:], offs3)
+        for t in range(PACK):
+            load_page(1, t)
+        with nc.allow_non_contiguous_dma(reason="one value of slot to a partition"):
+            nc.sync.dma_start(slot_t[:], slot.rearrange("(c p) -> p c", p=P))
+        nc.gpsimd.tensor_scalar(half_slot[:], slot_t[:], 0.5, 0.0, ALU.mult, ALU.add)
+
+        def dealt(bank):
+            return bank[:].rearrange("j (p t) -> j t p", t=PACK)
+
+        def products(b, jt, abs_slot, neg_slot, prod_slot):
+            cols = slice(jt * P, (jt + 1) * P)
+            r_cols = slice(b * PASS, (b + 1) * PASS)
+            bank_a = ps.tile([P, PASS], F32, name="bank_a", tag="A")
+            bank_b = ps.tile([P, PASS], F32, name="bank_b", tag="B")
+            bank_c = ps.tile([P, PASS], F32, name="bank_c", tag="C")
+            moving = (
+                (bank_b, [(w2_w[b][:, a, :].bitcast(FP4X4), w2_s[:, a, r_cols]) for a in range(2)]),
+                (bank_c, [(w3_w[b][:, a, :].bitcast(FP8X4), w3_s[W3_ROW:P, a, r_cols]) for a in range(2)]),
+                (bank_a, [(w1_q[a, b][0][:].bitcast(FP8X4), w1_q[a, b][1][:]) for a in range(2)]),
+            )
+            for bank, passes in moving:
+                order = (0, 1) if b == 0 else (1, 0)
+                for a in order:
+                    codes, scales = passes[a]
+                    nc.tensor.matmul_mx(
+                        out=bank[:], lhsT=v_w[a][:, cols].bitcast(FP8X4), lhsT_scale=v_s[a][:, cols],
+                        rhs=codes, rhs_scale=scales, start=(a == order[0]), stop=(a == order[1]),
+                    )
+            abs_b = new_tile([P, PACK, P], F32, "abs_b%d%d" % (b, jt), *abs_slot)
+            nc.scalar.activation(abs_b[:], dealt(bank_b), ACT.Abs)
+            neg_c = new_tile([P, PACK, P], F32, "neg_c%d%d" % (b, jt), *neg_slot)
+            nc.scalar.activation(neg_c[:], dealt(bank_c), ACT.Copy, scale=-1.0)
+            prod = new_tile([P, PACK, P], F32, "prod%d%d" % (b, jt), *prod_slot)
+            nc.vector.tensor_tensor(prod[:], dealt(bank_a), abs_b[:], ALU.mult)
+            return neg_c, prod
+
+        def turn(neg_c, prod):
+            bank_h = ps.tile([P, PACK, P], F32, name="bank_h", tag="H")
+            for t in range(PACK):
+                nc.tensor.matmul(bank_h[:, t, :], neg_c[:, t, :], ident[:], start=True, stop=False, is_transpose=True)
+                nc.tensor.matmul(bank_h[:, t, :], prod[:, t, :], ident[:], start=False, stop=True, is_transpose=True)
+            return bank_h
+
+        def put(b, t, h_part, j0, j1):
+            offsets = idx2[:] if j1 - j0 == S else idx2[:, j0 // 16 : j1 // 16]
+            nc.vector.tensor_tensor(
+                page[b][t][:].indirect(offsets), h_part, wg[t // 2][:, t % 2, j0:j1], ALU.mult
+            )
+
+        def fetch(b, t, x_bf, picked):
+            nc.vector.tensor_copy(picked, page[b][t][:].indirect(idx3[:]))
+            nc.vector.tensor_scalar(
+                x_bf[:, t, :], picked, low_t[:, b, t : t + 1], look_t[:, b, t : t + 1], ALU.max, ALU.mult
+            )
+
+        n_jt = S // P
+        h0_late = new_tile([P, 2, S], F32, "h0_late", "turn_h")
+        terms = [products(0, 0, ("wg2", 1), ("neg_c", 3), ("early0", 1))]
+        load_wg(nc.gpsimd, 2, "wg2")
+        for jt in range(n_jt):
+            cols = slice(jt * P, (jt + 1) * P)
+            if jt + 1 < n_jt:
+                prod_slot = ("early%d" % ((jt + 1) % 2), 1)
+                terms.append(products(0, jt + 1, ("abs_b", 2), ("neg_c", 3), prod_slot))
+            bank_h = turn(*terms[jt])
+            h0_early = new_tile([P, 2, P], F32, "h0_early%d" % jt, "early%d" % (jt % 2))
+            nc.scalar.copy(out=h0_early[:], in_=bank_h[:, 0:2, :])
+            nc.scalar.copy(out=h0_late[:, :, cols], in_=bank_h[:, 2:4, :])
+            for t in range(2):
+                put(0, t, h0_early[:, t, :], jt * P, (jt + 1) * P)
+        w1_q[0, 1] = quantize_w1(raw01, 0, 1, 0)
+        put(0, 2, h0_late[:, 0, :], 0, S)
+        w1_q[1, 1] = quantize_w1(raw11, 1, 1, 0)
+        put(0, 3, h0_late[:, 1, :], 0, S)
+
+        h1 = new_tile([P, PACK, S], F32, "h1")
+        x_bf0 = new_tile([P, PACK, NX], BF16, "x_bf0")
+        prod_slots = [("turn_h", 1), ("turn_h", 1), ("early0", 1), ("turn_page", 1)]
+        pick_tags = ["turn0", "turn2", "turn3", "turn1"]
+        terms = [products(1, 0, ("turn0", 1), ("neg_c", 3), prod_slots[0])]
+        for jt in range(n_jt):
+            if jt + 1 < n_jt:
+                terms.append(products(1, jt + 1, ("turn%d" % (jt + 1), 1), ("neg_c", 3), prod_slots[jt + 1]))
+            nc.scalar.copy(out=h1[:, :, jt * P : (jt + 1) * P], in_=turn(*terms[jt])[:])
+        for t in range(PACK):
+            fetch(0, t, x_bf0, new_tile([P, NX], F32, "picked0%d" % t, pick_tags[t])[:])
+
+        page_bf0 = new_tile([P, T2, PACK], BF16, "page_bf0", tag="turn_page")
+        for half in range(2):
+            cols = slice(half * PASS, (half + 1) * PASS)
+            joined = new_tile([P, PACK, PASS], F32, "joined%d" % half, tag="raw", bufs=2)
+            for t in range(PACK):
+                nc.sync.dma_start(joined[:, t, :], page[0][t][:, cols])
+            nc.scalar.copy(
+                out=page_bf0[:, cols, :].rearrange("p (c i) t -> p c t i", i=4),
+                in_=joined[:].rearrange("p t (c i) -> p c t i", i=4),
+            )
+        x_grouped0 = new_tile([P, NX, PACK], BF16, "x_grouped0", "raw", 2)
+        weave(nc.scalar.copy, x_grouped0, x_bf0, 0, NX)
+
+        page_bf1 = new_tile([P, T2, PACK], BF16, "page_bf1")
+        for t in range(PACK):
+            put(1, t, h1[:, t, :], 0, S)
+            nc.scalar.copy(out=page_bf1[:, :, t], in_=page[1][t][:])
+
+        page_q = [quantize(page_bf0, T2, "page_q0")]
+        x_q = [quantize(x_grouped0, NX, "x_q0")]
+
+        acc = [ps.tile([P, NX], F32, name="acc%d" % c, tag="BCAH"[c % 4]) for c in range(T2 // P)]
+
+        def compare(b, c):
+            cols = slice(c * P, (c + 1) * P)
+            nc.tensor.matmul_mx(
+                out=acc[c][:], lhsT=page_q[b][0][:, cols].bitcast(FP8X4), lhsT_scale=page_q[b][1][:, cols],
+                rhs=x_q[b][0][:].bitcast(FP8X4), rhs_scale=x_q[b][1][:], start=(b == 0), stop=(b == 1),
+            )
+
+        for c in range(T2 // P):
+            compare(0, c)
+
+        x_bf1 = new_tile([P, PACK, NX], BF16, "x_bf1")
+        picked1 = new_tile([P, PACK, NX], F32, "picked1", "turn_page")
+        for t in range(PACK):
+            fetch(1, t, x_bf1, picked1[:, t, :])
+        x_grouped1 = new_tile([P, NX, PACK], BF16, "x_grouped1")
+        weave(nc.scalar.copy, x_grouped1, x_bf1, X_VECTOR_COLS, NX)
+        page_q.append(quantize(page_bf1, T2, "page_q1"))
+        weave(nc.vector.tensor_copy, x_grouped1, x_bf1, 0, X_VECTOR_COLS)
+        x_q.append(quantize(x_grouped1, NX, "x_q1"))
+
+        mids = [new_tile([P, PACK, NX], F32, "mids%d" % u, "raw", 2) for u in range(2)]
+        results = [new_tile([P, PACK, NX], F32, "results%d" % u, tag) for u, tag in enumerate(("turn_page", "h1"))]
+        for c in range(T2 // P):
+            compare(1, c)
+            mid = mids[c // PACK][:, c % PACK, :]
+            result = results[c // PACK][:, c % PACK, :]
+            if c >= T2 // P - ABS_TILES:
+                nc.scalar.activation(mid, acc[c][:], ACT.Abs, bias=slot_t[:, c : c + 1])
+                nc.scalar.activation(result, mid, ACT.Sin, bias=math.pi / 2, scale=-1.0)
+            else:
+                nc.scalar.activation(mid, acc[c][:], ACT.Sin, bias=half_slot[:, c : c + 1], scale=0.5)
+                square = new_tile([P, NX], F32, "square%d" % c, tag="square", bufs=2)
+                nc.vector.scalar_tensor_tensor(square[:], mid, -2.0, mid, ALU.mult, ALU.mult)
+                nc.vector.tensor_scalar(result, square[:], 1.0, None, ALU.add)
+            nc.sync.dma_start(out[c * P : (c + 1) * P, :], result)

@@ -22,9 +22,8 @@ P = 128
 PACK = 4
 PASS = P * PACK
 W3_ROW = 4
-W1_VECTOR_COLS = 336
-X_VECTOR_COLS = 192
-ABS_TILES = 3
+CHUNKS = ((0, 256), (256, 512))
+ABS_BANKS = (4, 1)
 
 
 def weave(engine_copy, dst, src, c0, c1):
@@ -52,10 +51,11 @@ def tile_list_mix_slot_readout_kernel(
         idx3 = lists.tile([P, NX // 16], U16, name="idx3")
 
         tab_w = [new_tile([P, T], I32, "tab_w%d" % a) for a in range(2)]
-        wg = []
+        wg = [new_tile([P, 2, S], F32, "wg%d" % pair) for pair in range(2)]
         tab_s = new_tile([P, 2, T], U8, "tab_s")
         w2_s = new_tile([P, 2, H], U8, "w2_s")
         w3_s = new_tile([P, 2, H], U8, "w3_s")
+        warm = new_tile([P, 2], F32, "warm")
         w2_w = [new_tile([P, 2, 2 * PASS], U8, "w2_w%d" % b) for b in range(2)]
         w3_w = [new_tile([P, 2, PASS], U32, "w3_w%d" % b) for b in range(2)]
         page = [[new_tile([P, T2], F32, "page%d%d" % (b, t)) for t in range(PACK)] for b in range(2)]
@@ -69,16 +69,18 @@ def tile_list_mix_slot_readout_kernel(
             nc.sync.dma_start(tab_w[a][:], tab_words[a].rearrange("p n i -> p (n i)").bitcast(I32))
 
         def load_scales(queue, plane, row0, scales):
-            for q in range(4):
+            for q in (0, 2, 1, 3):
                 queue.dma_start(
                     plane[32 * q + row0 : 32 * q + row0 + 4].bitcast(I32),
                     scales[:, 4 * q : 4 * q + 4, :].rearrange("a r n -> r a n").bitcast(I32),
                 )
 
-        def load_w1(a, b):
+        def load_w1(a, b, pieces=1):
             raw = new_tile([P, PACK, PASS], F32, "w1_raw%d%d" % (a, b), tag="raw", bufs=2)
             rows = w1[a * PASS : (a + 1) * PASS, b * PASS : (b + 1) * PASS]
-            nc.sync.dma_start(raw[:], rows.rearrange("(p i) c -> p i c", i=PACK))
+            for c0 in range(0, PASS, PASS // pieces):
+                cols = slice(c0, c0 + PASS // pieces)
+                nc.sync.dma_start(raw[:, :, cols], rows.rearrange("(p i) c -> p i c", i=PACK)[:, :, cols])
             return raw
 
         def load_w23(b):
@@ -91,87 +93,100 @@ def tile_list_mix_slot_readout_kernel(
                 w3_words[:, :, b * PASS : (b + 1) * PASS, :].rearrange("a p n i -> p a (n i)").bitcast(I32),
             )
 
-        def load_wg(queue, t0, tag):
-            wg.append(new_tile([P, 2, S], F32, "wg%d" % t0, tag))
-            for q in range(4):
+        def load_wg(queue, pair, j0, j1):
+            for q in (0, 2, 1, 3):
                 queue.dma_start(
-                    wg[-1][32 * q : 32 * q + 32],
-                    wgs.rearrange("(p t) j -> p t j", t=PACK)[:, t0 : t0 + 2, :],
+                    wg[pair][32 * q : 32 * q + 32, :, j0:j1],
+                    wgs.rearrange("(p t) j -> p t j", t=PACK)[:, 2 * pair : 2 * pair + 2, j0:j1],
                 )
 
         def load_page(b, t):
             rows = page0[b * PASS : (b + 1) * PASS, :].rearrange("(p t) m -> p t m", t=PACK)
             nc.sync.dma_start(page[b][t][:], rows[:, t, :])
 
-        def quantize(grouped, width, name):
-            codes = new_tile([P, width], U32, name + "_c")
-            scales = new_tile([P, width], U8, name + "_s")
-            nc.vector.quantize_mx(
-                out=codes[:].bitcast(FP8X4), scales=scales[:], in_=grouped[:].rearrange("p c t -> p (c t)")
-            )
-            return codes, scales
+        def mx_tiles(width, name, tag=None):
+            return new_tile([P, width], U32, name + "_c", tag), new_tile([P, width], U8, name + "_s")
 
-        def quantize_w1(raw, a, b, vector_cols, slot_of=("w1_bf", 2)):
-            grouped = new_tile([P, PASS, PACK], BF16, "w1_bf%d%d" % (a, b), *slot_of)
-            if vector_cols:
-                weave(nc.vector.tensor_copy, grouped, raw, 0, vector_cols)
-            step = P if vector_cols == 0 else PASS - vector_cols
-            for c0 in range(vector_cols, PASS, step):
-                weave(nc.scalar.copy, grouped, raw, c0, c0 + step)
-            return quantize(grouped, PASS, "w1_%d%d" % (a, b))
+        def quantize_into(operand, cols, grouped):
+            nc.vector.quantize_mx(
+                out=operand[0][:, cols].bitcast(FP8X4), scales=operand[1][:, cols],
+                in_=grouped[:].rearrange("p c t -> p (c t)"),
+            )
+
+        def quantize(grouped, width, name, tag=None):
+            operand = mx_tiles(width, name, tag)
+            quantize_into(operand, slice(0, width), grouped)
+            return operand
+
+        def quantize_w1_early(raw, a, tags):
+            operand = mx_tiles(PASS, "w1_%d0" % a)
+            width = PASS // len(tags)
+            for u, tag in enumerate(tags):
+                cols = slice(u * width, (u + 1) * width)
+                grouped = new_tile([P, width, PACK], BF16, "w1_bf%d0%d" % (a, u), tag)
+                weave(nc.vector.tensor_copy, grouped, raw[:, :, cols], 0, width)
+                quantize_into(operand, cols, grouped)
+            return operand
+
+        def quantize_w1_late(raw, a):
+            grouped = new_tile([P, PASS, PACK], BF16, "w1_bf%d1" % a)
+            for c0 in range(0, PASS, P):
+                weave(nc.scalar.copy, grouped, raw, c0, c0 + P)
+            return quantize(grouped, PASS, "w1_%d1" % a)
 
         nc.vector.memset(tab_s[:].bitcast(I32), 0)
         nc.gpsimd.memset(w2_s[:].bitcast(I32), 0)
         nc.vector.memset(w3_s[:].bitcast(I32), 0)
+        nc.vector.memset(warm[:, 0:1], 0.0)
+        nc.scalar.activation(warm[:, 1:2], warm[:, 0:1], ACT.Sin)
         nc.sync.dma_start(idx[:], offs)
         load_table_words(0)
         load_scales(nc.sync, tab_s, 0, tab_scales)
-        raw00 = load_w1(0, 0)
         load_table_words(1)
-        raw10 = load_w1(1, 0)
+        raw00 = load_w1(0, 0)
         load_w23(0)
+        raw10 = load_w1(1, 0, 2)
         load_scales(nc.gpsimd, w2_s, 0, w2_scales)
         load_scales(nc.gpsimd, w3_s, W3_ROW, w3_scales)
         make_identity(nc, ident[:])
         nc.sync.dma_start(idx2[:], offs2)
         load_page(0, 0)
+        load_wg(nc.sync, 0, 0, P)
         load_page(0, 1)
-        load_wg(nc.sync, 0, "wg0")
+        load_wg(nc.sync, 0, P, S)
         nc.gpsimd.dma_start(low_t[:], low.rearrange("(b p t) -> p b t", b=2, t=PACK))
         nc.gpsimd.dma_start(look_t[:], look.rearrange("(b p t) -> p b t", b=2, t=PACK))
 
         v_w, v_s = [], []
         w1_q = {}
-        for a, raw in ((0, raw00), (1, raw10)):
+        for a in range(2):
             words = new_tile([P, S], U32, "v_w%d" % a)
             nc.vector.tensor_copy(words[:], tab_w[a][:].bitcast(U32).indirect(idx[:]))
             planes = new_tile([P, S], U8, "v_s%d" % a)
             nc.vector.tensor_copy(planes[:], tab_s[:, a, :].indirect(idx[:]))
             v_w.append(words)
             v_s.append(planes)
-            w1_q[a, 0] = quantize_w1(raw, a, 0, W1_VECTOR_COLS)
+        w1_q[0, 0] = quantize_w1_early(raw00, 0, ["w1_bf01"])
+        w1_q[1, 0] = quantize_w1_early(raw10, 1, ["turn_a", "turn_n"])
 
+        load_wg(nc.sync, 1, 0, S)
         raw01 = load_w1(0, 1)
         load_page(0, 2)
         raw11 = load_w1(1, 1)
         load_w23(1)
-        load_page(0, 3)
         nc.sync.dma_start(idx3[:], offs3)
-        for t in range(PACK):
-            load_page(1, t)
-        with nc.allow_non_contiguous_dma(reason="one value of slot to a partition"):
-            nc.sync.dma_start(slot_t[:], slot.rearrange("(c p) -> p c", p=P))
-        nc.gpsimd.tensor_scalar(half_slot[:], slot_t[:], 0.5, 0.0, ALU.mult, ALU.add)
+        load_page(1, 0)
+        load_page(0, 3)
 
         def dealt(bank):
             return bank[:].rearrange("j (p t) -> j t p", t=PACK)
 
-        def products(b, jt, abs_slot, neg_slot, prod_slot):
+        def products(b, jt, abs_slot, neg_slot, prod_slot, parts=((0, PACK),)):
             cols = slice(jt * P, (jt + 1) * P)
             r_cols = slice(b * PASS, (b + 1) * PASS)
             bank_a = ps.tile([P, PASS], F32, name="bank_a", tag="A")
-            bank_b = ps.tile([P, PASS], F32, name="bank_b", tag="B")
-            bank_c = ps.tile([P, PASS], F32, name="bank_c", tag="C")
+            bank_b = ps.tile([P, PASS], F32, name="bank_b", tag="B%d" % (b * jt % 2), bufs=1)
+            bank_c = ps.tile([P, PASS], F32, name="bank_c", tag="C%d" % (b * jt % 2), bufs=1)
             moving = (
                 (bank_b, [(w2_w[b][:, a, :].bitcast(FP4X4), w2_s[:, a, r_cols]) for a in range(2)]),
                 (bank_c, [(w3_w[b][:, a, :].bitcast(FP8X4), w3_s[W3_ROW:P, a, r_cols]) for a in range(2)]),
@@ -188,14 +203,16 @@ def tile_list_mix_slot_readout_kernel(
             abs_b = new_tile([P, PACK, P], F32, "abs_b%d%d" % (b, jt), *abs_slot)
             nc.scalar.activation(abs_b[:], dealt(bank_b), ACT.Abs)
             neg_c = new_tile([P, PACK, P], F32, "neg_c%d%d" % (b, jt), *neg_slot)
-            nc.scalar.activation(neg_c[:], dealt(bank_c), ACT.Copy, scale=-1.0)
+            for t0, t1 in parts:
+                nc.scalar.activation(neg_c[:, t0:t1, :], dealt(bank_c)[:, t0:t1, :], ACT.Copy, scale=-1.0)
             prod = new_tile([P, PACK, P], F32, "prod%d%d" % (b, jt), *prod_slot)
-            nc.vector.tensor_tensor(prod[:], dealt(bank_a), abs_b[:], ALU.mult)
+            for t0, t1 in parts:
+                nc.vector.tensor_tensor(prod[:, t0:t1, :], dealt(bank_a)[:, t0:t1, :], abs_b[:, t0:t1, :], ALU.mult)
             return neg_c, prod
 
-        def turn(neg_c, prod):
+        def turn(neg_c, prod, t0=0, t1=PACK):
             bank_h = ps.tile([P, PACK, P], F32, name="bank_h", tag="H")
-            for t in range(PACK):
+            for t in range(t0, t1):
                 nc.tensor.matmul(bank_h[:, t, :], neg_c[:, t, :], ident[:], start=True, stop=False, is_transpose=True)
                 nc.tensor.matmul(bank_h[:, t, :], prod[:, t, :], ident[:], start=False, stop=True, is_transpose=True)
             return bank_h
@@ -206,99 +223,123 @@ def tile_list_mix_slot_readout_kernel(
                 page[b][t][:].indirect(offsets), h_part, wg[t // 2][:, t % 2, j0:j1], ALU.mult
             )
 
-        def fetch(b, t, x_bf, picked):
-            nc.vector.tensor_copy(picked, page[b][t][:].indirect(idx3[:]))
+        def fetch(b, t, j0, j1, x_bf, picked):
+            offsets = idx3[:] if j1 - j0 == NX else idx3[:, j0 // 16 : j1 // 16]
+            nc.vector.tensor_copy(picked, page[b][t][:].indirect(offsets))
             nc.vector.tensor_scalar(
                 x_bf[:, t, :], picked, low_t[:, b, t : t + 1], look_t[:, b, t : t + 1], ALU.max, ALU.mult
             )
 
         n_jt = S // P
         h0_late = new_tile([P, 2, S], F32, "h0_late", "turn_h")
-        terms = [products(0, 0, ("wg2", 1), ("neg_c", 3), ("early0", 1))]
-        load_wg(nc.gpsimd, 2, "wg2")
+        abs_slots = [("abs_b", 2), ("turn_a", 1), ("turn_p", 1), ("abs_b", 2)]
+        neg_slots = [("neg_c", 4), ("turn_n", 1), ("neg_c", 4), ("neg_c", 4)]
+        prod_slots = [("early0", 1), ("early1", 1), ("early0", 1), ("turn_p", 1)]
+        terms = [products(0, 0, abs_slots[0], ("neg_c", 4), prod_slots[0], ((0, 1), (1, PACK)))]
+        h0_first = new_tile([P, P], F32, "h0_first")
+        nc.scalar.copy(out=h0_first[:], in_=turn(*terms[0], 0, 1)[:, 0, :])
+        put(0, 0, h0_first[:], 0, P)
         for jt in range(n_jt):
             cols = slice(jt * P, (jt + 1) * P)
             if jt + 1 < n_jt:
-                prod_slot = ("early%d" % ((jt + 1) % 2), 1)
-                terms.append(products(0, jt + 1, ("abs_b", 2), ("neg_c", 3), prod_slot))
-            bank_h = turn(*terms[jt])
+                terms.append(products(0, jt + 1, abs_slots[jt + 1], neg_slots[jt + 1], prod_slots[jt + 1]))
+            t0 = 0 if jt else 1
+            bank_h = turn(*terms[jt], t0)
             h0_early = new_tile([P, 2, P], F32, "h0_early%d" % jt, "early%d" % (jt % 2))
-            nc.scalar.copy(out=h0_early[:], in_=bank_h[:, 0:2, :])
+            nc.scalar.copy(out=h0_early[:, t0:2, :], in_=bank_h[:, t0:2, :])
             nc.scalar.copy(out=h0_late[:, :, cols], in_=bank_h[:, 2:4, :])
-            for t in range(2):
+            for t in range(t0, 2):
                 put(0, t, h0_early[:, t, :], jt * P, (jt + 1) * P)
-        w1_q[0, 1] = quantize_w1(raw01, 0, 1, 0)
+        w1_q[0, 1] = quantize_w1_late(raw01, 0)
         put(0, 2, h0_late[:, 0, :], 0, S)
-        w1_q[1, 1] = quantize_w1(raw11, 1, 1, 0)
+        w1_q[1, 1] = quantize_w1_late(raw11, 1)
         put(0, 3, h0_late[:, 1, :], 0, S)
 
+        widths = [j1 - j0 for j0, j1 in CHUNKS]
         h1 = new_tile([P, PACK, S], F32, "h1")
         x_bf0 = new_tile([P, PACK, NX], BF16, "x_bf0")
-        prod_slots = [("turn_h", 1), ("turn_h", 1), ("early0", 1), ("turn_page", 1)]
+        prod_slots = [("turn_h", 1), ("turn_h", 1), ("early0", 1), ("early1", 1)]
         pick_tags = ["turn0", "turn2", "turn3", "turn1"]
-        terms = [products(1, 0, ("turn0", 1), ("neg_c", 3), prod_slots[0])]
+        terms = [products(1, 0, ("turn0", 1), ("neg_c", 4), prod_slots[0])]
         for jt in range(n_jt):
             if jt + 1 < n_jt:
-                terms.append(products(1, jt + 1, ("turn%d" % (jt + 1), 1), ("neg_c", 3), prod_slots[jt + 1]))
+                terms.append(products(1, jt + 1, ("turn%d" % (jt + 1), 1), ("neg_c", 4), prod_slots[jt + 1]))
             nc.scalar.copy(out=h1[:, :, jt * P : (jt + 1) * P], in_=turn(*terms[jt])[:])
         for t in range(PACK):
-            fetch(0, t, x_bf0, new_tile([P, NX], F32, "picked0%d" % t, pick_tags[t])[:])
+            fetch(0, t, 0, NX, x_bf0, new_tile([P, NX], F32, "picked0%d" % t, pick_tags[t])[:])
 
         page_bf0 = new_tile([P, T2, PACK], BF16, "page_bf0", tag="turn_page")
         for half in range(2):
-            cols = slice(half * PASS, (half + 1) * PASS)
             joined = new_tile([P, PACK, PASS], F32, "joined%d" % half, tag="raw", bufs=2)
             for t in range(PACK):
-                nc.sync.dma_start(joined[:, t, :], page[0][t][:, cols])
-            nc.scalar.copy(
-                out=page_bf0[:, cols, :].rearrange("p (c i) t -> p c t i", i=4),
-                in_=joined[:].rearrange("p t (c i) -> p c t i", i=4),
-            )
-        x_grouped0 = new_tile([P, NX, PACK], BF16, "x_grouped0", "raw", 2)
-        weave(nc.scalar.copy, x_grouped0, x_bf0, 0, NX)
+                nc.sync.dma_start(joined[:, t, :], page[0][t][:, half * PASS : (half + 1) * PASS])
+            for c0 in range(0, PASS, P):
+                weave(nc.scalar.copy, page_bf0[:, half * PASS : (half + 1) * PASS, :], joined, c0, c0 + P)
+        for t in range(1, PACK):
+            load_page(1, t)
+        with nc.allow_non_contiguous_dma(reason="one value of slot to a partition"):
+            nc.sync.dma_start(slot_t[:], slot.rearrange("(c p) -> p c", p=P))
+        nc.gpsimd.tensor_scalar(half_slot[:], slot_t[:], 0.5, 0.0, ALU.mult, ALU.add)
 
+        x_grouped0 = new_tile([P, NX, PACK], BF16, "x_grouped0")
+        for c0 in range(0, NX, P):
+            weave(nc.scalar.copy, x_grouped0, x_bf0, c0, c0 + P)
         page_bf1 = new_tile([P, T2, PACK], BF16, "page_bf1")
         for t in range(PACK):
             put(1, t, h1[:, t, :], 0, S)
             nc.scalar.copy(out=page_bf1[:, :, t], in_=page[1][t][:])
 
         page_q = [quantize(page_bf0, T2, "page_q0")]
-        x_q = [quantize(x_grouped0, NX, "x_q0")]
+        x_q = [quantize(x_grouped0, NX, "x_q0"), mx_tiles(NX, "x_q1")]
+        bank_slots = [("B0", 1), ("C0", 1), ("B1", 1), ("C1", 1), ("A", 2), ("A", 2), ("H", 2), ("H", 2)]
 
-        acc = [ps.tile([P, NX], F32, name="acc%d" % c, tag="BCAH"[c % 4]) for c in range(T2 // P)]
+        acc = {}
 
-        def compare(b, c):
+        def compare(b, u, c):
+            if b == 0:
+                acc[u, c] = ps.tile([P, widths[u]], F32, name="acc", tag=bank_slots[c][0], bufs=bank_slots[c][1])
             cols = slice(c * P, (c + 1) * P)
+            picks = slice(*CHUNKS[u])
             nc.tensor.matmul_mx(
-                out=acc[c][:], lhsT=page_q[b][0][:, cols].bitcast(FP8X4), lhsT_scale=page_q[b][1][:, cols],
-                rhs=x_q[b][0][:].bitcast(FP8X4), rhs_scale=x_q[b][1][:], start=(b == 0), stop=(b == 1),
+                out=acc[u, c][:], lhsT=page_q[b][0][:, cols].bitcast(FP8X4), lhsT_scale=page_q[b][1][:, cols],
+                rhs=x_q[b][0][:, picks].bitcast(FP8X4), rhs_scale=x_q[b][1][:, picks], start=(b == 0), stop=(b == 1),
             )
 
-        for c in range(T2 // P):
-            compare(0, c)
+        def read_out(u):
+            j0, j1 = CHUNKS[u]
+            side = PASS // widths[u]
+            n_groups = T2 // P // side
+            for k in range(n_groups):
+                mid = new_tile([P, side, widths[u]], F32, "mid%d%d" % (u, k), "mid", 4)
+                result = new_tile([P, side, widths[u]], F32, "result%d%d" % (u, k), "result", 6)
+                by_abs = k >= n_groups - ABS_BANKS[u]
+                for s in range(side):
+                    c = k * side + s
+                    compare(1, u, c)
+                    if by_abs:
+                        nc.scalar.activation(mid[:, s, :], acc[u, c][:], ACT.Abs, bias=slot_t[:, c : c + 1])
+                    else:
+                        nc.scalar.activation(mid[:, s, :], acc[u, c][:], ACT.Sin, bias=half_slot[:, c : c + 1], scale=0.5)
+                if by_abs:
+                    nc.scalar.activation(result[:], mid[:], ACT.Sin, bias=math.pi / 2, scale=-1.0)
+                else:
+                    square = new_tile([P, side, widths[u]], F32, "square%d%d" % (u, k), "square", 2)
+                    nc.vector.scalar_tensor_tensor(square[:], mid[:], -2.0, mid[:], ALU.mult, ALU.mult)
+                    nc.vector.tensor_scalar(result[:], square[:], 1.0, None, ALU.add)
+                rows = out[k * side * P : (k + 1) * side * P, j0:j1]
+                nc.sync.dma_start(rows.rearrange("(s p) j -> p s j", p=P), result[:])
 
-        x_bf1 = new_tile([P, PACK, NX], BF16, "x_bf1")
-        picked1 = new_tile([P, PACK, NX], F32, "picked1", "turn_page")
-        for t in range(PACK):
-            fetch(1, t, x_bf1, picked1[:, t, :])
-        x_grouped1 = new_tile([P, NX, PACK], BF16, "x_grouped1")
-        weave(nc.scalar.copy, x_grouped1, x_bf1, X_VECTOR_COLS, NX)
-        page_q.append(quantize(page_bf1, T2, "page_q1"))
-        weave(nc.vector.tensor_copy, x_grouped1, x_bf1, 0, X_VECTOR_COLS)
-        x_q.append(quantize(x_grouped1, NX, "x_q1"))
-
-        mids = [new_tile([P, PACK, NX], F32, "mids%d" % u, "raw", 2) for u in range(2)]
-        results = [new_tile([P, PACK, NX], F32, "results%d" % u, tag) for u, tag in enumerate(("turn_page", "h1"))]
-        for c in range(T2 // P):
-            compare(1, c)
-            mid = mids[c // PACK][:, c % PACK, :]
-            result = results[c // PACK][:, c % PACK, :]
-            if c >= T2 // P - ABS_TILES:
-                nc.scalar.activation(mid, acc[c][:], ACT.Abs, bias=slot_t[:, c : c + 1])
-                nc.scalar.activation(result, mid, ACT.Sin, bias=math.pi / 2, scale=-1.0)
-            else:
-                nc.scalar.activation(mid, acc[c][:], ACT.Sin, bias=half_slot[:, c : c + 1], scale=0.5)
-                square = new_tile([P, NX], F32, "square%d" % c, tag="square", bufs=2)
-                nc.vector.scalar_tensor_tensor(square[:], mid, -2.0, mid, ALU.mult, ALU.mult)
-                nc.vector.tensor_scalar(result, square[:], 1.0, None, ALU.add)
-            nc.sync.dma_start(out[c * P : (c + 1) * P, :], result)
+        last = len(CHUNKS) - 1
+        for u, (j0, j1) in enumerate(CHUNKS):
+            for c in range(T2 // P):
+                compare(0, u, c)
+            picked = new_tile([P, PACK, widths[u]], F32, "picked1%d" % u, "turn_x%d" % (u - 1) if u else "turn_page")
+            x_bf1 = new_tile([P, PACK, widths[u]], BF16, "x_bf1%d" % u)
+            for t in range(PACK):
+                fetch(1, t, j0, j1, x_bf1, picked[:, t, :])
+            x_grouped1 = new_tile([P, widths[u], PACK], BF16, "x_grouped1%d" % u, "turn_x%d" % u)
+            weave(nc.vector.tensor_copy if u == last else nc.scalar.copy, x_grouped1, x_bf1, 0, widths[u])
+            if u == 0:
+                page_q.append(quantize(page_bf1, T2, "page_q1"))
+            quantize_into(x_q[1], slice(j0, j1), x_grouped1)
+            read_out(u)

@@ -23,7 +23,8 @@ PACK = 4
 PASS = P * PACK
 W3_ROW = 4
 CHUNKS = ((0, 256), (256, 512))
-ABS_BANKS = (4, 1)
+X_VECTOR_COLS = 64
+ROADS = (("scalar",) * 4, ("fold", "square", "square", "scalar"))
 
 
 def weave(engine_copy, dst, src, c0, c1):
@@ -118,13 +119,16 @@ def tile_list_mix_slot_readout_kernel(
             quantize_into(operand, slice(0, width), grouped)
             return operand
 
-        def quantize_w1_early(raw, a, tags):
+        def quantize_w1_early(raw, a, tags, shared):
             operand = mx_tiles(PASS, "w1_%d0" % a)
             width = PASS // len(tags)
             for u, tag in enumerate(tags):
                 cols = slice(u * width, (u + 1) * width)
                 grouped = new_tile([P, width, PACK], BF16, "w1_bf%d0%d" % (a, u), tag)
-                weave(nc.vector.tensor_copy, grouped, raw[:, :, cols], 0, width)
+                cut = width * 2 // 3 // 4 * 4 if shared[u] else width
+                weave(nc.vector.tensor_copy, grouped, raw[:, :, cols], 0, cut)
+                if cut < width:
+                    weave(nc.scalar.copy, grouped, raw[:, :, cols], cut, width)
                 quantize_into(operand, cols, grouped)
             return operand
 
@@ -143,19 +147,17 @@ def tile_list_mix_slot_readout_kernel(
         load_table_words(0)
         load_scales(nc.sync, tab_s, 0, tab_scales)
         load_table_words(1)
-        raw00 = load_w1(0, 0)
+        load_scales(nc.sync, w3_s, W3_ROW, w3_scales)
         load_w23(0)
+        raw00 = load_w1(0, 0)
         raw10 = load_w1(1, 0, 2)
         load_scales(nc.gpsimd, w2_s, 0, w2_scales)
-        load_scales(nc.gpsimd, w3_s, W3_ROW, w3_scales)
         make_identity(nc, ident[:])
         nc.sync.dma_start(idx2[:], offs2)
         load_page(0, 0)
         load_wg(nc.sync, 0, 0, P)
         load_page(0, 1)
         load_wg(nc.sync, 0, P, S)
-        nc.gpsimd.dma_start(low_t[:], low.rearrange("(b p t) -> p b t", b=2, t=PACK))
-        nc.gpsimd.dma_start(look_t[:], look.rearrange("(b p t) -> p b t", b=2, t=PACK))
 
         v_w, v_s = [], []
         w1_q = {}
@@ -166,8 +168,8 @@ def tile_list_mix_slot_readout_kernel(
             nc.vector.tensor_copy(planes[:], tab_s[:, a, :].indirect(idx[:]))
             v_w.append(words)
             v_s.append(planes)
-        w1_q[0, 0] = quantize_w1_early(raw00, 0, ["w1_bf01"])
-        w1_q[1, 0] = quantize_w1_early(raw10, 1, ["turn_a", "turn_n"])
+        w1_q[0, 0] = quantize_w1_early(raw00, 0, ["w1_bf01"], [True])
+        w1_q[1, 0] = quantize_w1_early(raw10, 1, ["w1_bf11", "turn_n"], [False, True])
 
         load_wg(nc.sync, 1, 0, S)
         raw01 = load_w1(0, 1)
@@ -175,13 +177,18 @@ def tile_list_mix_slot_readout_kernel(
         raw11 = load_w1(1, 1)
         load_w23(1)
         nc.sync.dma_start(idx3[:], offs3)
-        load_page(1, 0)
+        nc.sync.dma_start(low_t[:], low.rearrange("(b p t) -> p b t", b=2, t=PACK))
         load_page(0, 3)
+        nc.sync.dma_start(look_t[:], look.rearrange("(b p t) -> p b t", b=2, t=PACK))
+        load_page(1, 0)
 
         def dealt(bank):
             return bank[:].rearrange("j (p t) -> j t p", t=PACK)
 
-        def products(b, jt, abs_slot, neg_slot, prod_slot, parts=((0, PACK),)):
+        def term(name, tag, bufs=1):
+            return new_tile([P, PACK, P], F32, name, tag, bufs)[:]
+
+        def products(b, jt, abs_b, neg_c, prod, parts=((0, PACK),)):
             cols = slice(jt * P, (jt + 1) * P)
             r_cols = slice(b * PASS, (b + 1) * PASS)
             bank_a = ps.tile([P, PASS], F32, name="bank_a", tag="A")
@@ -200,12 +207,9 @@ def tile_list_mix_slot_readout_kernel(
                         out=bank[:], lhsT=v_w[a][:, cols].bitcast(FP8X4), lhsT_scale=v_s[a][:, cols],
                         rhs=codes, rhs_scale=scales, start=(a == order[0]), stop=(a == order[1]),
                     )
-            abs_b = new_tile([P, PACK, P], F32, "abs_b%d%d" % (b, jt), *abs_slot)
-            nc.scalar.activation(abs_b[:], dealt(bank_b), ACT.Abs)
-            neg_c = new_tile([P, PACK, P], F32, "neg_c%d%d" % (b, jt), *neg_slot)
+            nc.scalar.activation(abs_b, dealt(bank_b), ACT.Abs)
             for t0, t1 in parts:
                 nc.scalar.activation(neg_c[:, t0:t1, :], dealt(bank_c)[:, t0:t1, :], ACT.Copy, scale=-1.0)
-            prod = new_tile([P, PACK, P], F32, "prod%d%d" % (b, jt), *prod_slot)
             for t0, t1 in parts:
                 nc.vector.tensor_tensor(prod[:, t0:t1, :], dealt(bank_a)[:, t0:t1, :], abs_b[:, t0:t1, :], ALU.mult)
             return neg_c, prod
@@ -223,33 +227,41 @@ def tile_list_mix_slot_readout_kernel(
                 page[b][t][:].indirect(offsets), h_part, wg[t // 2][:, t % 2, j0:j1], ALU.mult
             )
 
-        def fetch(b, t, j0, j1, x_bf, picked):
+        def fetch(b, ts, j0, j1, x_bf, picked):
             offsets = idx3[:] if j1 - j0 == NX else idx3[:, j0 // 16 : j1 // 16]
-            nc.vector.tensor_copy(picked, page[b][t][:].indirect(offsets))
-            nc.vector.tensor_scalar(
-                x_bf[:, t, :], picked, low_t[:, b, t : t + 1], look_t[:, b, t : t + 1], ALU.max, ALU.mult
-            )
+            for n, t in enumerate(ts):
+                nc.vector.tensor_copy(picked[:, n, :], page[b][t][:].indirect(offsets))
+            for n, t in enumerate(ts):
+                nc.vector.tensor_scalar(
+                    x_bf[:, t, :], picked[:, n, :], low_t[:, b, t : t + 1], look_t[:, b, t : t + 1], ALU.max, ALU.mult
+                )
 
         n_jt = S // P
         h0_late = new_tile([P, 2, S], F32, "h0_late", "turn_h")
-        abs_slots = [("abs_b", 2), ("turn_a", 1), ("turn_p", 1), ("abs_b", 2)]
-        neg_slots = [("neg_c", 4), ("turn_n", 1), ("neg_c", 4), ("neg_c", 4)]
-        prod_slots = [("early0", 1), ("early1", 1), ("early0", 1), ("turn_p", 1)]
-        terms = [products(0, 0, abs_slots[0], ("neg_c", 4), prod_slots[0], ((0, 1), (1, PACK)))]
-        h0_first = new_tile([P, P], F32, "h0_first")
-        nc.scalar.copy(out=h0_first[:], in_=turn(*terms[0], 0, 1)[:, 0, :])
-        put(0, 0, h0_first[:], 0, P)
+
+        def first_half_terms(jt):
+            prod = term("prod0%d" % jt, "early%d" % (jt % 2))
+            if jt == 1:
+                both = new_tile([P, 2, PACK, P], F32, "terms01", "turn_n")
+                return products(0, jt, both[:, 0], both[:, 1], prod)
+            parts = ((0, PACK),) if jt else ((0, 1), (1, PACK))
+            return products(0, jt, term("abs_b0%d" % jt, "abs_b", 2), term("neg_c0%d" % jt, "neg_c", 4), prod, parts)
+
+        def put_early(jt, t, bank_h, tag):
+            h_early = new_tile([P, P], F32, "h0_early%d%d" % (jt, t), tag)
+            nc.scalar.copy(out=h_early[:], in_=bank_h[:, t, :])
+            put(0, t, h_early[:], jt * P, (jt + 1) * P)
+
+        terms = [first_half_terms(0)]
+        put_early(0, 0, turn(*terms[0], 0, 1), None)
         for jt in range(n_jt):
-            cols = slice(jt * P, (jt + 1) * P)
             if jt + 1 < n_jt:
-                terms.append(products(0, jt + 1, abs_slots[jt + 1], neg_slots[jt + 1], prod_slots[jt + 1]))
+                terms.append(first_half_terms(jt + 1))
             t0 = 0 if jt else 1
             bank_h = turn(*terms[jt], t0)
-            h0_early = new_tile([P, 2, P], F32, "h0_early%d" % jt, "early%d" % (jt % 2))
-            nc.scalar.copy(out=h0_early[:, t0:2, :], in_=bank_h[:, t0:2, :])
-            nc.scalar.copy(out=h0_late[:, :, cols], in_=bank_h[:, 2:4, :])
             for t in range(t0, 2):
-                put(0, t, h0_early[:, t, :], jt * P, (jt + 1) * P)
+                put_early(jt, t, bank_h, "early%d" % jt if jt + t == 1 else None)
+            nc.scalar.copy(out=h0_late[:, :, jt * P : (jt + 1) * P], in_=bank_h[:, 2:4, :])
         w1_q[0, 1] = quantize_w1_late(raw01, 0)
         put(0, 2, h0_late[:, 0, :], 0, S)
         w1_q[1, 1] = quantize_w1_late(raw11, 1)
@@ -258,15 +270,20 @@ def tile_list_mix_slot_readout_kernel(
         widths = [j1 - j0 for j0, j1 in CHUNKS]
         h1 = new_tile([P, PACK, S], F32, "h1")
         x_bf0 = new_tile([P, PACK, NX], BF16, "x_bf0")
-        prod_slots = [("turn_h", 1), ("turn_h", 1), ("early0", 1), ("early1", 1)]
-        pick_tags = ["turn0", "turn2", "turn3", "turn1"]
-        terms = [products(1, 0, ("turn0", 1), ("neg_c", 4), prod_slots[0])]
+        held = new_tile([P, 2, PACK, P], F32, "prod1_held", "turn_h")
+        prods = [held[:, 0], held[:, 1], term("prod12", "early0"), term("prod13", "early1")]
+
+        def second_half_terms(jt):
+            abs_b = term("abs_b1%d" % jt, "turn%d" % jt)
+            return products(1, jt, abs_b, term("neg_c1%d" % jt, "neg_c", 4), prods[jt])
+
+        terms = [second_half_terms(0)]
         for jt in range(n_jt):
             if jt + 1 < n_jt:
-                terms.append(products(1, jt + 1, ("turn%d" % (jt + 1), 1), ("neg_c", 4), prod_slots[jt + 1]))
+                terms.append(second_half_terms(jt + 1))
             nc.scalar.copy(out=h1[:, :, jt * P : (jt + 1) * P], in_=turn(*terms[jt])[:])
-        for t in range(PACK):
-            fetch(0, t, 0, NX, x_bf0, new_tile([P, NX], F32, "picked0%d" % t, pick_tags[t])[:])
+        for ts, tag in (((0, 1), "turn0"), ((2, 3), "turn3")):
+            fetch(0, ts, 0, NX, x_bf0, new_tile([P, 2, NX], F32, "picked0%d" % ts[0], tag))
 
         page_bf0 = new_tile([P, T2, PACK], BF16, "page_bf0", tag="turn_page")
         for half in range(2):
@@ -281,16 +298,23 @@ def tile_list_mix_slot_readout_kernel(
             nc.sync.dma_start(slot_t[:], slot.rearrange("(c p) -> p c", p=P))
         nc.gpsimd.tensor_scalar(half_slot[:], slot_t[:], 0.5, 0.0, ALU.mult, ALU.add)
 
-        x_grouped0 = new_tile([P, NX, PACK], BF16, "x_grouped0")
-        for c0 in range(0, NX, P):
-            weave(nc.scalar.copy, x_grouped0, x_bf0, c0, c0 + P)
+        x_q = [mx_tiles(NX, "x_q%d" % b) for b in range(2)]
+
+        def group_first_half(u, tag):
+            j0, j1 = CHUNKS[u]
+            grouped = new_tile([P, j1 - j0, PACK], BF16, "x_grouped0%d" % u, tag)
+            for c0 in range(0, j1 - j0, P):
+                weave(nc.scalar.copy, grouped, x_bf0[:, :, j0:j1], c0, c0 + P)
+            return grouped
+
+        x_grouped0 = group_first_half(0, None)
         page_bf1 = new_tile([P, T2, PACK], BF16, "page_bf1")
         for t in range(PACK):
             put(1, t, h1[:, t, :], 0, S)
             nc.scalar.copy(out=page_bf1[:, :, t], in_=page[1][t][:])
 
         page_q = [quantize(page_bf0, T2, "page_q0")]
-        x_q = [quantize(x_grouped0, NX, "x_q0"), mx_tiles(NX, "x_q1")]
+        quantize_into(x_q[0], slice(*CHUNKS[0]), x_grouped0)
         bank_slots = [("B0", 1), ("C0", 1), ("B1", 1), ("C1", 1), ("A", 2), ("A", 2), ("H", 2), ("H", 2)]
 
         acc = {}
@@ -312,34 +336,49 @@ def tile_list_mix_slot_readout_kernel(
             for k in range(n_groups):
                 mid = new_tile([P, side, widths[u]], F32, "mid%d%d" % (u, k), "mid", 4)
                 result = new_tile([P, side, widths[u]], F32, "result%d%d" % (u, k), "result", 6)
-                by_abs = k >= n_groups - ABS_BANKS[u]
+                road = ROADS[u][k]
+                spare = None if road == "scalar" else new_tile([P, side, widths[u]], F32, "spare%d%d" % (u, k), "spare", 2)
                 for s in range(side):
                     c = k * side + s
                     compare(1, u, c)
-                    if by_abs:
+                    if road == "scalar":
                         nc.scalar.activation(mid[:, s, :], acc[u, c][:], ACT.Abs, bias=slot_t[:, c : c + 1])
+                    elif road == "fold":
+                        nc.vector.tensor_scalar(spare[:, s, :], acc[u, c][:], slot_t[:, c : c + 1], None, ALU.add)
                     else:
                         nc.scalar.activation(mid[:, s, :], acc[u, c][:], ACT.Sin, bias=half_slot[:, c : c + 1], scale=0.5)
-                if by_abs:
-                    nc.scalar.activation(result[:], mid[:], ACT.Sin, bias=math.pi / 2, scale=-1.0)
+                if road == "square":
+                    nc.vector.scalar_tensor_tensor(spare[:], mid[:], -2.0, mid[:], ALU.mult, ALU.mult)
+                    nc.vector.tensor_scalar(result[:], spare[:], 1.0, None, ALU.add)
                 else:
-                    square = new_tile([P, side, widths[u]], F32, "square%d%d" % (u, k), "square", 2)
-                    nc.vector.scalar_tensor_tensor(square[:], mid[:], -2.0, mid[:], ALU.mult, ALU.mult)
-                    nc.vector.tensor_scalar(result[:], square[:], 1.0, None, ALU.add)
+                    if road == "fold":
+                        nc.vector.scalar_tensor_tensor(mid[:], spare[:], -1.0, spare[:], ALU.mult, ALU.max)
+                    nc.scalar.activation(result[:], mid[:], ACT.Sin, bias=math.pi / 2, scale=-1.0)
                 rows = out[k * side * P : (k + 1) * side * P, j0:j1]
                 nc.sync.dma_start(rows.rearrange("(s p) j -> p s j", p=P), result[:])
 
-        last = len(CHUNKS) - 1
-        for u, (j0, j1) in enumerate(CHUNKS):
-            for c in range(T2 // P):
-                compare(0, u, c)
-            picked = new_tile([P, PACK, widths[u]], F32, "picked1%d" % u, "turn_x%d" % (u - 1) if u else "turn_page")
-            x_bf1 = new_tile([P, PACK, widths[u]], BF16, "x_bf1%d" % u)
-            for t in range(PACK):
-                fetch(1, t, j0, j1, x_bf1, picked[:, t, :])
-            x_grouped1 = new_tile([P, widths[u], PACK], BF16, "x_grouped1%d" % u, "turn_x%d" % u)
-            weave(nc.vector.tensor_copy if u == last else nc.scalar.copy, x_grouped1, x_bf1, 0, widths[u])
-            if u == 0:
-                page_q.append(quantize(page_bf1, T2, "page_q1"))
-            quantize_into(x_q[1], slice(j0, j1), x_grouped1)
-            read_out(u)
+        (j0, j1), (j1, j2) = CHUNKS
+        for c in range(T2 // P):
+            compare(0, 0, c)
+        x_bf1 = new_tile([P, PACK, j1 - j0], BF16, "x_bf10", "turn_y")
+        fetch(1, range(PACK), j0, j1, x_bf1, new_tile([P, PACK, j1 - j0], F32, "picked10", "turn_page"))
+        x_grouped1 = new_tile([P, j1 - j0, PACK], BF16, "x_grouped10", "turn_x")
+        weave(nc.scalar.copy, x_grouped1, x_bf1, X_VECTOR_COLS, j1 - j0)
+        page_q.append(quantize(page_bf1, T2, "page_q1"))
+        weave(nc.vector.tensor_copy, x_grouped1, x_bf1, 0, X_VECTOR_COLS)
+        quantize_into(x_q[1], slice(j0, j1), x_grouped1)
+        x_grouped0 = group_first_half(1, "turn_y")
+        read_out(0)
+
+        x_bf1 = new_tile([P, PACK, j2 - j1], BF16, "x_bf11")
+        fetch(1, range(PACK), j1, j2, x_bf1, new_tile([P, PACK, j2 - j1], F32, "picked11", "turn_x"))
+        quantize_into(x_q[0], slice(j1, j2), x_grouped0)
+        for c in range(T2 // P):
+            compare(0, 1, c)
+        x_grouped1 = new_tile([P, j2 - j1, PACK], BF16, "x_grouped11")
+        halves = [slice(c0, c0 + P) for c0 in range(0, j2 - j1, P)]
+        for cols in halves:
+            weave(nc.vector.tensor_copy, x_grouped1, x_bf1, cols.start, cols.stop)
+        for cols in halves:
+            quantize_into(x_q[1], slice(j1 + cols.start, j1 + cols.stop), x_grouped1[:, cols, :])
+        read_out(1)

@@ -24,7 +24,9 @@ PASS = P * PACK
 W3_ROW = 4
 CHUNKS = ((0, 256), (256, 512))
 X_VECTOR_COLS = 64
-ROADS = (("scalar",) * 4, ("fold", "square", "square", "scalar"))
+FIRST_TAGS = (("early0", "early1", "early0", "early1"), ("h0_0", "early1", "early0", "h0_1"))
+VW0_TAG = None
+ROADS = (("scalar", "scalar", "scalar", "fold"), ("fold", "square", "square", "scalar"))
 
 
 def weave(engine_copy, dst, src, c0, c1):
@@ -51,23 +53,27 @@ def tile_list_mix_slot_readout_kernel(
         idx2 = lists.tile([P, S // 16], U16, name="idx2")
         idx3 = lists.tile([P, NX // 16], U16, name="idx3")
 
-        tab_w = [new_tile([P, T], I32, "tab_w%d" % a) for a in range(2)]
-        wg = [new_tile([P, 2, S], F32, "wg%d" % pair) for pair in range(2)]
-        tab_s = new_tile([P, 2, T], U8, "tab_s")
+        n_ct = PASS // P
+        n_jt = S // P
+        tab_w = new_tile([P, 2, T], I32, "tab_w", tag="wide")
+        tab_s = new_tile([P, 2, T], U8, "tab_s", tag="tab_s")
         w2_s = new_tile([P, 2, H], U8, "w2_s")
         w3_s = new_tile([P, 2, H], U8, "w3_s")
         warm = new_tile([P, 2], F32, "warm")
-        w2_w = [new_tile([P, 2, 2 * PASS], U8, "w2_w%d" % b) for b in range(2)]
-        w3_w = [new_tile([P, 2, PASS], U32, "w3_w%d" % b) for b in range(2)]
+        wg_rows = new_tile([P, S], F32, "wg_rows")
+        wg_dealt = new_tile([P, PACK, S], F32, "wg_dealt")
+        r_parts = ((0, P), (P, 2 * P), (2 * P, PASS), (PASS, H))
+        w2_w = [new_tile([P, 2, 2 * (r1 - r0)], U8, "w2_w%d" % r0) for r0, r1 in r_parts]
+        w3_w = [new_tile([P, 2, r1 - r0], U32, "w3_w%d" % r0) for r0, r1 in r_parts]
         page = [[new_tile([P, T2], F32, "page%d%d" % (b, t)) for t in range(PACK)] for b in range(2)]
-        low_t = new_tile([P, 2, PACK], F32, "low_t")
-        look_t = new_tile([P, 2, PACK], F32, "look_t")
+        low_t = [new_tile([P, PACK], F32, "low_t%d" % b) for b in range(2)]
+        look_t = [new_tile([P, PACK], F32, "look_t%d" % b) for b in range(2)]
         slot_t = new_tile([P, T2 // P], F32, "slot_t")
         half_slot = new_tile([P, T2 // P], F32, "half_slot")
         ident = new_tile([P, P], F32, "ident")
 
         def load_table_words(a):
-            nc.sync.dma_start(tab_w[a][:], tab_words[a].rearrange("p n i -> p (n i)").bitcast(I32))
+            nc.sync.dma_start(tab_w[:, a, :], tab_words[a].rearrange("p n i -> p (n i)").bitcast(I32))
 
         def load_scales(queue, plane, row0, scales):
             for q in (0, 2, 1, 3):
@@ -76,34 +82,30 @@ def tile_list_mix_slot_readout_kernel(
                     scales[:, 4 * q : 4 * q + 4, :].rearrange("a r n -> r a n").bitcast(I32),
                 )
 
-        def load_w1(a, b, pieces=1):
-            raw = new_tile([P, PACK, PASS], F32, "w1_raw%d%d" % (a, b), tag="raw", bufs=2)
-            rows = w1[a * PASS : (a + 1) * PASS, b * PASS : (b + 1) * PASS]
-            for c0 in range(0, PASS, PASS // pieces):
-                cols = slice(c0, c0 + PASS // pieces)
-                nc.sync.dma_start(raw[:, :, cols], rows.rearrange("(p i) c -> p i c", i=PACK)[:, :, cols])
+        def load_w1(a, r0, r1, tag, bufs):
+            raw = new_tile([P, PACK, r1 - r0], F32, "w1_raw%d_%d" % (a, r0), tag, bufs)
+            rows = w1[a * PASS : (a + 1) * PASS, r0:r1]
+            nc.sync.dma_start(raw[:], rows.rearrange("(p i) c -> p i c", i=PACK))
             return raw
 
-        def load_w23(b):
+        def load_w2(part):
+            r0, r1 = r_parts[part]
             nc.sync.dma_start(
-                w2_w[b][:].bitcast(I32),
-                w2_words[:, :, 2 * b * PASS : 2 * (b + 1) * PASS].rearrange("a p n -> p a n").bitcast(I32),
-            )
-            nc.sync.dma_start(
-                w3_w[b][:].bitcast(I32),
-                w3_words[:, :, b * PASS : (b + 1) * PASS, :].rearrange("a p n i -> p a (n i)").bitcast(I32),
+                w2_w[part][:].bitcast(I32), w2_words[:, :, 2 * r0 : 2 * r1].rearrange("a p n -> p a n").bitcast(I32)
             )
 
-        def load_wg(queue, pair, j0, j1):
-            for q in (0, 2, 1, 3):
-                queue.dma_start(
-                    wg[pair][32 * q : 32 * q + 32, :, j0:j1],
-                    wgs.rearrange("(p t) j -> p t j", t=PACK)[:, 2 * pair : 2 * pair + 2, j0:j1],
-                )
+        def load_w3(part):
+            r0, r1 = r_parts[part]
+            nc.sync.dma_start(
+                w3_w[part][:].bitcast(I32), w3_words[:, :, r0:r1, :].rearrange("a p n i -> p a (n i)").bitcast(I32)
+            )
 
         def load_page(b, t):
-            rows = page0[b * PASS : (b + 1) * PASS, :].rearrange("(p t) m -> p t m", t=PACK)
-            nc.sync.dma_start(page[b][t][:], rows[:, t, :])
+            rows = page0[b * PASS : (b + 1) * PASS, :]
+            if b == 0:
+                nc.sync.dma_start(page[b][t][:], rows[t * P : (t + 1) * P, :])
+            else:
+                nc.sync.dma_start(page[b][t][:], rows.rearrange("(p t) m -> p t m", t=PACK)[:, t, :])
 
         def mx_tiles(width, name, tag=None):
             return new_tile([P, width], U32, name + "_c", tag), new_tile([P, width], U8, name + "_s")
@@ -119,24 +121,13 @@ def tile_list_mix_slot_readout_kernel(
             quantize_into(operand, slice(0, width), grouped)
             return operand
 
-        def quantize_w1_early(raw, a, tags, shared):
-            operand = mx_tiles(PASS, "w1_%d0" % a)
-            width = PASS // len(tags)
-            for u, tag in enumerate(tags):
-                cols = slice(u * width, (u + 1) * width)
-                grouped = new_tile([P, width, PACK], BF16, "w1_bf%d0%d" % (a, u), tag)
-                cut = width * 2 // 3 // 4 * 4 if shared[u] else width
-                weave(nc.vector.tensor_copy, grouped, raw[:, :, cols], 0, cut)
-                if cut < width:
-                    weave(nc.scalar.copy, grouped, raw[:, :, cols], cut, width)
-                quantize_into(operand, cols, grouped)
-            return operand
+        w1_q = [mx_tiles(H, "w1_q%d" % a) for a in range(2)]
 
-        def quantize_w1_late(raw, a):
-            grouped = new_tile([P, PASS, PACK], BF16, "w1_bf%d1" % a)
-            for c0 in range(0, PASS, P):
-                weave(nc.scalar.copy, grouped, raw, c0, c0 + P)
-            return quantize(grouped, PASS, "w1_%d1" % a)
+        def group_w1(copy, raw, a, r0, r1, tag, bufs=1):
+            grouped = new_tile([P, r1 - r0, PACK], BF16, "w1_bf%d_%d" % (a, r0), tag, bufs)
+            for c0 in range(0, r1 - r0, P):
+                weave(copy, grouped, raw, c0, c0 + P)
+            return grouped
 
         nc.vector.memset(tab_s[:].bitcast(I32), 0)
         nc.gpsimd.memset(w2_s[:].bitcast(I32), 0)
@@ -144,43 +135,108 @@ def tile_list_mix_slot_readout_kernel(
         nc.vector.memset(warm[:, 0:1], 0.0)
         nc.scalar.activation(warm[:, 1:2], warm[:, 0:1], ACT.Sin)
         nc.sync.dma_start(idx[:], offs)
-        load_table_words(0)
+        raw = {}
+        raw[0, 0] = load_w1(0, 0, P, "raw_small", 4)
+        load_w2(0)
         load_scales(nc.sync, tab_s, 0, tab_scales)
+        load_table_words(0)
         load_table_words(1)
+        load_scales(nc.sync, w2_s, 0, w2_scales)
+        raw[1, 0] = load_w1(1, 0, P, "raw_small", 4)
+        load_w3(0)
         load_scales(nc.sync, w3_s, W3_ROW, w3_scales)
-        load_w23(0)
-        raw00 = load_w1(0, 0)
-        raw10 = load_w1(1, 0, 2)
-        load_scales(nc.gpsimd, w2_s, 0, w2_scales)
-        make_identity(nc, ident[:])
-        nc.sync.dma_start(idx2[:], offs2)
         load_page(0, 0)
-        load_wg(nc.sync, 0, 0, P)
-        load_page(0, 1)
-        load_wg(nc.sync, 0, P, S)
-
-        v_w, v_s = [], []
-        w1_q = {}
-        for a in range(2):
-            words = new_tile([P, S], U32, "v_w%d" % a)
-            nc.vector.tensor_copy(words[:], tab_w[a][:].bitcast(U32).indirect(idx[:]))
-            planes = new_tile([P, S], U8, "v_s%d" % a)
-            nc.vector.tensor_copy(planes[:], tab_s[:, a, :].indirect(idx[:]))
-            v_w.append(words)
-            v_s.append(planes)
-        w1_q[0, 0] = quantize_w1_early(raw00, 0, ["w1_bf01"], [True])
-        w1_q[1, 0] = quantize_w1_early(raw10, 1, ["w1_bf11", "turn_n"], [False, True])
-
-        load_wg(nc.sync, 1, 0, S)
-        raw01 = load_w1(0, 1)
-        load_page(0, 2)
-        raw11 = load_w1(1, 1)
-        load_w23(1)
+        nc.sync.dma_start(wg_rows[:, 0 : S // 2], wgs[:, 0 : S // 2])
+        nc.sync.dma_start(idx2[:], offs2)
+        make_identity(nc, ident[:])
+        raw[0, 1] = load_w1(0, P, 2 * P, "raw_small", 4)
+        raw[1, 1] = load_w1(1, P, 2 * P, "raw_small", 4)
+        load_w2(1)
+        nc.sync.dma_start(wg_rows[:, S // 2 : S], wgs[:, S // 2 : S])
+        load_w3(1)
+        raw[0, 2] = load_w1(0, 2 * P, PASS, "raw_mid", 2)
         nc.sync.dma_start(idx3[:], offs3)
-        nc.sync.dma_start(low_t[:], low.rearrange("(b p t) -> p b t", b=2, t=PACK))
+        raw[1, 2] = load_w1(1, 2 * P, PASS, "raw_mid", 2)
+        load_w2(2)
+        load_w3(2)
+        load_page(0, 1)
+        raw01 = load_w1(0, PASS, H, "raw", 1)
+        load_page(0, 2)
+        raw11 = load_w1(1, PASS, H, "raw_b", 1)
+        load_w2(3)
+        load_w3(3)
+        with nc.allow_non_contiguous_dma(reason="one value to a partition"):
+            nc.sync.dma_start(low_t[0][:], low[0:PASS].rearrange("(c p) -> p c", p=P))
+            nc.sync.dma_start(look_t[0][:], look[0:PASS].rearrange("(c p) -> p c", p=P))
+        nc.sync.dma_start(low_t[1][:], low[PASS:H].rearrange("(p t) -> p t", t=PACK))
+        nc.sync.dma_start(look_t[1][:], look[PASS:H].rearrange("(p t) -> p t", t=PACK))
         load_page(0, 3)
-        nc.sync.dma_start(look_t[:], look.rearrange("(b p t) -> p b t", b=2, t=PACK))
-        load_page(1, 0)
+        for q in (0, 2, 1, 3):
+            nc.sync.dma_start(wg_dealt[32 * q : 32 * q + 32], wgs.rearrange("(p t) j -> p t j", t=PACK))
+        for t in range(PACK):
+            load_page(1, t)
+        with nc.allow_non_contiguous_dma(reason="one value of slot to a partition"):
+            nc.sync.dma_start(slot_t[:], slot.rearrange("(c p) -> p c", p=P))
+        nc.gpsimd.tensor_scalar(half_slot[:], slot_t[:], 0.5, 0.0, ALU.mult, ALU.add)
+
+        v_s = [new_tile([P, S], U8, "v_s%d" % a) for a in range(2)]
+        for a in range(2):
+            nc.vector.tensor_copy(v_s[a][:], tab_s[:, a, :].indirect(idx[:]))
+        v_w = [new_tile([P, S], U32, "v_w%d" % a, VW0_TAG if a == 0 else None) for a in range(2)]
+        nc.vector.tensor_copy(v_w[0][:], tab_w[:, 0, :].bitcast(U32).indirect(idx[:]))
+        for a in range(2):
+            quantize_into(w1_q[a], slice(0, P), group_w1(nc.vector.tensor_copy, raw[a, 0], a, 0, P, "bf_small", 2))
+        nc.vector.tensor_copy(v_w[1][:], tab_w[:, 1, :].bitcast(U32).indirect(idx[:]))
+
+        def weights(c):
+            cols = slice(c * P, (c + 1) * P)
+            part, c0 = min(c, 2), max(c - 2, 0) * P
+            return (
+                [(w2_w[part][:, a, 2 * c0 : 2 * (c0 + P)].bitcast(FP4X4), w2_s[:, a, cols]) for a in range(2)],
+                [(w3_w[part][:, a, c0 : c0 + P].bitcast(FP8X4), w3_s[W3_ROW:P, a, cols]) for a in range(2)],
+                [(w1_q[a][0][:, cols].bitcast(FP8X4), w1_q[a][1][:, cols]) for a in range(2)],
+            )
+
+        def three_banks(shape, n):
+            return (
+                ps.tile(shape, F32, name="bank_b", tag="B%d" % (n % 2), bufs=1),
+                ps.tile(shape, F32, name="bank_c", tag="C%d" % (n % 2), bufs=1),
+                ps.tile(shape, F32, name="bank_a", tag="A"),
+            )
+
+        def put(b, t, h_part, j0, j1):
+            offsets = idx2[:] if j1 - j0 == S else idx2[:, j0 // 16 : j1 // 16]
+            gains = wg_rows[:, j0:j1] if b == 0 else wg_dealt[:, t, j0:j1]
+            nc.vector.tensor_tensor(page[b][t][:].indirect(offsets), h_part, gains, ALU.mult)
+
+        def direct(c, parts):
+            banks = three_banks([P, S], c)
+            bank_b, bank_c, bank_a = banks
+            w_b, w_c, w_a = weights(c)
+            order = (1, 0) if c else (0, 1)
+            for bank, passes in ((bank_b, w_b), (bank_a, w_a), (bank_c, w_c)):
+                for a in order:
+                    nc.tensor.matmul_mx(
+                        out=bank[:], lhsT=passes[a][0], lhsT_scale=passes[a][1],
+                        rhs=v_w[a][:].bitcast(FP8X4), rhs_scale=v_s[a][:], start=(a == order[0]), stop=(a == order[1]),
+                    )
+            abs_b = new_tile([P, S], F32, "abs_b0%d" % c, "neg_c", 4)
+            prod = new_tile([P, S], F32, "prod0%d" % c, "early%d" % (c % 2))
+            h = new_tile([P, S], F32, "h0%d" % c, "h0_%d" % (c % 2))
+            for j0, j1 in parts:
+                nc.scalar.activation(abs_b[:, j0:j1], bank_b[:, j0:j1], ACT.Abs)
+            for j0, j1 in parts:
+                nc.vector.tensor_tensor(prod[:, j0:j1], bank_a[:, j0:j1], abs_b[:, j0:j1], ALU.mult)
+            for j0, j1 in parts:
+                nc.vector.tensor_tensor(h[:, j0:j1], prod[:, j0:j1], bank_c[:, j0:j1], ALU.subtract)
+            return h
+
+        def turn(neg_c, prod, tag):
+            bank_h = ps.tile([P, PACK, P], F32, name="bank_h", tag=tag)
+            for t in range(PACK):
+                nc.tensor.matmul(bank_h[:, t, :], neg_c[:, t, :], ident[:], start=True, stop=False, is_transpose=True)
+                nc.tensor.matmul(bank_h[:, t, :], prod[:, t, :], ident[:], start=False, stop=True, is_transpose=True)
+            return bank_h
 
         def dealt(bank):
             return bank[:].rearrange("j (p t) -> j t p", t=PACK)
@@ -188,197 +244,217 @@ def tile_list_mix_slot_readout_kernel(
         def term(name, tag, bufs=1):
             return new_tile([P, PACK, P], F32, name, tag, bufs)[:]
 
-        def products(b, jt, abs_b, neg_c, prod, parts=((0, PACK),)):
+        def products(jt, abs_b, neg_c, prod):
             cols = slice(jt * P, (jt + 1) * P)
-            r_cols = slice(b * PASS, (b + 1) * PASS)
-            bank_a = ps.tile([P, PASS], F32, name="bank_a", tag="A")
-            bank_b = ps.tile([P, PASS], F32, name="bank_b", tag="B%d" % (b * jt % 2), bufs=1)
-            bank_c = ps.tile([P, PASS], F32, name="bank_c", tag="C%d" % (b * jt % 2), bufs=1)
+            r_cols = slice(PASS, H)
+            bank_b, bank_c, bank_a = three_banks([P, PASS], jt)
             moving = (
-                (bank_b, [(w2_w[b][:, a, :].bitcast(FP4X4), w2_s[:, a, r_cols]) for a in range(2)]),
-                (bank_c, [(w3_w[b][:, a, :].bitcast(FP8X4), w3_s[W3_ROW:P, a, r_cols]) for a in range(2)]),
-                (bank_a, [(w1_q[a, b][0][:].bitcast(FP8X4), w1_q[a, b][1][:]) for a in range(2)]),
+                (bank_b, [(w2_w[3][:, a, :].bitcast(FP4X4), w2_s[:, a, r_cols]) for a in range(2)]),
+                (bank_c, [(w3_w[3][:, a, :].bitcast(FP8X4), w3_s[W3_ROW:P, a, r_cols]) for a in range(2)]),
+                (bank_a, [(w1_q[a][0][:, r_cols].bitcast(FP8X4), w1_q[a][1][:, r_cols]) for a in range(2)]),
             )
             for bank, passes in moving:
-                order = (0, 1) if b == 0 else (1, 0)
-                for a in order:
+                for a in (1, 0):
                     codes, scales = passes[a]
                     nc.tensor.matmul_mx(
                         out=bank[:], lhsT=v_w[a][:, cols].bitcast(FP8X4), lhsT_scale=v_s[a][:, cols],
-                        rhs=codes, rhs_scale=scales, start=(a == order[0]), stop=(a == order[1]),
+                        rhs=codes, rhs_scale=scales, start=(a == 1), stop=(a == 0),
                     )
             nc.scalar.activation(abs_b, dealt(bank_b), ACT.Abs)
-            for t0, t1 in parts:
-                nc.scalar.activation(neg_c[:, t0:t1, :], dealt(bank_c)[:, t0:t1, :], ACT.Copy, scale=-1.0)
-            for t0, t1 in parts:
-                nc.vector.tensor_tensor(prod[:, t0:t1, :], dealt(bank_a)[:, t0:t1, :], abs_b[:, t0:t1, :], ALU.mult)
+            nc.scalar.activation(neg_c, dealt(bank_c), ACT.Copy, scale=-1.0)
+            nc.vector.tensor_tensor(prod, dealt(bank_a), abs_b, ALU.mult)
             return neg_c, prod
 
-        def turn(neg_c, prod, t0=0, t1=PACK):
-            bank_h = ps.tile([P, PACK, P], F32, name="bank_h", tag="H")
-            for t in range(t0, t1):
-                nc.tensor.matmul(bank_h[:, t, :], neg_c[:, t, :], ident[:], start=True, stop=False, is_transpose=True)
-                nc.tensor.matmul(bank_h[:, t, :], prod[:, t, :], ident[:], start=False, stop=True, is_transpose=True)
-            return bank_h
-
-        def put(b, t, h_part, j0, j1):
-            offsets = idx2[:] if j1 - j0 == S else idx2[:, j0 // 16 : j1 // 16]
-            nc.vector.tensor_tensor(
-                page[b][t][:].indirect(offsets), h_part, wg[t // 2][:, t % 2, j0:j1], ALU.mult
-            )
-
-        def fetch(b, ts, j0, j1, x_bf, picked):
+        def pick(b, ts, j0, j1, picked):
             offsets = idx3[:] if j1 - j0 == NX else idx3[:, j0 // 16 : j1 // 16]
             for n, t in enumerate(ts):
                 nc.vector.tensor_copy(picked[:, n, :], page[b][t][:].indirect(offsets))
+
+        def clamp(b, ts, x_bf, picked):
             for n, t in enumerate(ts):
                 nc.vector.tensor_scalar(
-                    x_bf[:, t, :], picked[:, n, :], low_t[:, b, t : t + 1], look_t[:, b, t : t + 1], ALU.max, ALU.mult
+                    x_bf[:, t, :], picked[:, n, :], low_t[b][:, t : t + 1], look_t[b][:, t : t + 1], ALU.max, ALU.mult
                 )
 
-        n_jt = S // P
-        h0_late = new_tile([P, 2, S], F32, "h0_late", "turn_h")
+        page_across = new_tile([P, T2 // P, 2, P, 2], BF16, "page_across", "wide")
+        x_bf0 = new_tile([P, PACK, NX], BF16, "x_bf0")
 
-        def first_half_terms(jt):
-            prod = term("prod0%d" % jt, "early%d" % (jt % 2))
-            if jt == 1:
-                both = new_tile([P, 2, PACK, P], F32, "terms01", "turn_n")
-                return products(0, jt, both[:, 0], both[:, 1], prod)
-            parts = ((0, PACK),) if jt else ((0, 1), (1, PACK))
-            return products(0, jt, term("abs_b0%d" % jt, "abs_b", 2), term("neg_c0%d" % jt, "neg_c", 4), prod, parts)
+        def page_rows_across(c, tags=(("H", 2), ("H", 2))):
+            for m0, (tag, bufs) in zip(range(0, T2 // P, PACK), tags):
+                bank = ps.tile([P, PACK, P], F32, name="bank_t", tag=tag, bufs=bufs)
+                for i in range(PACK):
+                    nc.tensor.transpose(bank[:, i, :], page[0][c][:, (m0 + i) * P : (m0 + i + 1) * P], ident[:])
+                nc.scalar.copy(
+                    out=page_across[:, m0 : m0 + PACK, :, 32 * c : 32 * c + 32, :],
+                    in_=bank[:].rearrange("m i (p h e) -> m i h p e", h=2, e=2),
+                )
 
-        def put_early(jt, t, bank_h, tag):
-            h_early = new_tile([P, P], F32, "h0_early%d%d" % (jt, t), tag)
-            nc.scalar.copy(out=h_early[:], in_=bank_h[:, t, :])
-            put(0, t, h_early[:], jt * P, (jt + 1) * P)
+        def back_down(across, i0, grouped, tag, bufs):
+            words = across[:].rearrange("m i h p e -> m i h (p e)").bitcast(F32)
+            bank = ps.tile([P, 2, 2, P], F32, name="bank_w", tag=tag, bufs=bufs)
+            for i in range(2):
+                for h in range(2):
+                    nc.tensor.transpose(bank[:, i, h, :], words[:, i0 + i, h, :], ident[:])
+            nc.scalar.copy(
+                out=grouped.rearrange("p (i m) t -> p i (m t)", i=2).bitcast(F32).rearrange("p i (m h) -> p i m h", h=2),
+                in_=bank[:].rearrange("p i h m -> p i m h"),
+            )
 
-        terms = [first_half_terms(0)]
-        put_early(0, 0, turn(*terms[0], 0, 1), None)
-        for jt in range(n_jt):
-            if jt + 1 < n_jt:
-                terms.append(first_half_terms(jt + 1))
-            t0 = 0 if jt else 1
-            bank_h = turn(*terms[jt], t0)
-            for t in range(t0, 2):
-                put_early(jt, t, bank_h, "early%d" % jt if jt + t == 1 else None)
-            nc.scalar.copy(out=h0_late[:, :, jt * P : (jt + 1) * P], in_=bank_h[:, 2:4, :])
-        w1_q[0, 1] = quantize_w1_late(raw01, 0)
-        put(0, 2, h0_late[:, 0, :], 0, S)
-        w1_q[1, 1] = quantize_w1_late(raw11, 1)
-        put(0, 3, h0_late[:, 1, :], 0, S)
+        halves = ((0, S // 2), (S // 2, S))
+        h_first = direct(0, halves)
+        put(0, 0, h_first[:, 0 : S // 2], *halves[0])
+        for a in range(2):
+            quantize_into(w1_q[a], slice(P, 2 * P), group_w1(nc.scalar.copy, raw[a, 1], a, P, 2 * P, "bf1%d" % a))
+        put(0, 0, h_first[:, S // 2 : S], *halves[1])
+        h_second = direct(1, halves)
+        picked = [new_tile([P, 1, NX], F32, "picked00")]
+        pick(0, (0,), 0, NX, picked[0])
+        for a in range(2):
+            quantize_into(w1_q[a], slice(2 * P, PASS), group_w1(nc.scalar.copy, raw[a, 2], a, 2 * P, PASS, "bf2%d" % a))
+        put(0, 1, h_second[:], 0, S)
+        h_third = direct(2, halves)
+        h_fourth = direct(3, halves)
+        late = [group_w1(nc.scalar.copy, raw_late, a, PASS, H, "bf_late%d" % a) for a, raw_late in enumerate((raw01, raw11))]
+        page_rows_across(0, (("B0", 1), ("B1", 1)))
+        put(0, 2, h_third[:], 0, S)
+        page_rows_across(1, (("C0", 1), ("C1", 1)))
+        for a in range(2):
+            quantize_into(w1_q[a], slice(PASS, H), late[a])
+        clamp(0, (0,), x_bf0, picked[0])
+        put(0, 3, h_fourth[:], 0, S)
 
         widths = [j1 - j0 for j0, j1 in CHUNKS]
-        h1 = new_tile([P, PACK, S], F32, "h1")
-        x_bf0 = new_tile([P, PACK, NX], BF16, "x_bf0")
-        held = new_tile([P, 2, PACK, P], F32, "prod1_held", "turn_h")
+        h1 = new_tile([P, PACK, S], F32, "h1", "raw")
+        held = new_tile([P, 2, PACK, P], F32, "prod1_held", "wg_rows")
         prods = [held[:, 0], held[:, 1], term("prod12", "early0"), term("prod13", "early1")]
 
         def second_half_terms(jt):
             abs_b = term("abs_b1%d" % jt, "turn%d" % jt)
-            return products(1, jt, abs_b, term("neg_c1%d" % jt, "neg_c", 4), prods[jt])
+            return products(jt, abs_b, term("neg_c1%d" % jt, "neg_c", 4), prods[jt])
 
-        terms = [second_half_terms(0)]
+        terms = [second_half_terms(jt) for jt in range(n_jt)]
+        page_rows_across(2, (("B0", 1), ("C0", 1)))
         for jt in range(n_jt):
-            if jt + 1 < n_jt:
-                terms.append(second_half_terms(jt + 1))
-            nc.scalar.copy(out=h1[:, :, jt * P : (jt + 1) * P], in_=turn(*terms[jt])[:])
-        for ts, tag in (((0, 1), "turn0"), ((2, 3), "turn3")):
-            fetch(0, ts, 0, NX, x_bf0, new_tile([P, 2, NX], F32, "picked0%d" % ts[0], tag))
-
+            nc.scalar.copy(out=h1[:, :, jt * P : (jt + 1) * P], in_=turn(*terms[jt], "H" if jt < 2 else "A")[:])
+        page_rows_across(3, (("B1", 1), ("C1", 1)))
+        picked = [new_tile([P, 1, NX], F32, "picked01", "turn1"), new_tile([P, 2, NX], F32, "picked02", "turn3")]
+        pick(0, (1,), 0, NX, picked[0])
+        pick(0, (2, 3), 0, NX, picked[1])
+        clamp(0, (1,), x_bf0, picked[0])
+        clamp(0, (2, 3), x_bf0, picked[1])
         page_bf0 = new_tile([P, T2, PACK], BF16, "page_bf0", tag="turn_page")
-        for half in range(2):
-            joined = new_tile([P, PACK, PASS], F32, "joined%d" % half, tag="raw", bufs=2)
+        for n, tag in enumerate(("B0", "C0", "B1", "C1")):
+            back_down(page_across, 2 * n, page_bf0[:, 2 * n * P : 2 * (n + 1) * P, :], tag, 1)
+        x_joined = new_tile([P, PACK, NX], BF16, "x_joined")
+        for c in (0, 2, 1, 3):
             for t in range(PACK):
-                nc.sync.dma_start(joined[:, t, :], page[0][t][:, half * PASS : (half + 1) * PASS])
-            for c0 in range(0, PASS, P):
-                weave(nc.scalar.copy, page_bf0[:, half * PASS : (half + 1) * PASS, :], joined, c0, c0 + P)
-        for t in range(1, PACK):
-            load_page(1, t)
-        with nc.allow_non_contiguous_dma(reason="one value of slot to a partition"):
-            nc.sync.dma_start(slot_t[:], slot.rearrange("(c p) -> p c", p=P))
-        nc.gpsimd.tensor_scalar(half_slot[:], slot_t[:], 0.5, 0.0, ALU.mult, ALU.add)
+                nc.sync.dma_start(x_joined[32 * c : 32 * c + 32, t, :], x_bf0[t:P:PACK, c, :])
 
-        x_q = [mx_tiles(NX, "x_q%d" % b) for b in range(2)]
+        codes0 = new_tile([P, T2 + NX], U32, "codes0", "wg_dealt")
+        x_q = [(codes0[:, T2 : T2 + NX], new_tile([P, NX], U8, "x_q0_s")), mx_tiles(NX, "x_q1")]
+        page_q = [(codes0[:, 0:T2], new_tile([P, T2], U8, "page_q0_s")), mx_tiles(T2, "page_q1")]
 
-        def group_first_half(u, tag):
-            j0, j1 = CHUNKS[u]
-            grouped = new_tile([P, j1 - j0, PACK], BF16, "x_grouped0%d" % u, tag)
-            for c0 in range(0, j1 - j0, P):
-                weave(nc.scalar.copy, grouped, x_bf0[:, :, j0:j1], c0, c0 + P)
-            return grouped
-
-        x_grouped0 = group_first_half(0, None)
-        page_bf1 = new_tile([P, T2, PACK], BF16, "page_bf1")
+        page_bf1 = new_tile([P, T2, PACK], BF16, "page_bf1", "wide")
         for t in range(PACK):
             put(1, t, h1[:, t, :], 0, S)
             nc.scalar.copy(out=page_bf1[:, :, t], in_=page[1][t][:])
 
-        page_q = [quantize(page_bf0, T2, "page_q0")]
-        quantize_into(x_q[0], slice(*CHUNKS[0]), x_grouped0)
         bank_slots = [("B0", 1), ("C0", 1), ("B1", 1), ("C1", 1), ("A", 2), ("A", 2), ("H", 2), ("H", 2)]
 
         acc = {}
 
         def compare(b, u, c):
-            if b == 0:
+            first = b == 0
+            if first:
                 acc[u, c] = ps.tile([P, widths[u]], F32, name="acc", tag=bank_slots[c][0], bufs=bank_slots[c][1])
             cols = slice(c * P, (c + 1) * P)
             picks = slice(*CHUNKS[u])
             nc.tensor.matmul_mx(
                 out=acc[u, c][:], lhsT=page_q[b][0][:, cols].bitcast(FP8X4), lhsT_scale=page_q[b][1][:, cols],
-                rhs=x_q[b][0][:, picks].bitcast(FP8X4), rhs_scale=x_q[b][1][:, picks], start=(b == 0), stop=(b == 1),
+                rhs=x_q[b][0][:, picks].bitcast(FP8X4), rhs_scale=x_q[b][1][:, picks], start=first, stop=not first,
             )
 
-        def read_out(u):
+        def open_group(u, k, first):
+            side = PASS // widths[u]
+            road = ROADS[u][k]
+            for s in range(side):
+                c = k * side + s
+                if u == 0:
+                    compare(0, u, c)
+                compare(1, u, c)
+                if road == "scalar":
+                    nc.scalar.activation(first[:, s, :], acc[u, c][:], ACT.Abs, bias=slot_t[:, c : c + 1])
+                elif road == "fold":
+                    nc.vector.tensor_scalar(first[:, s, :], acc[u, c][:], slot_t[:, c : c + 1], None, ALU.add)
+                else:
+                    nc.scalar.activation(first[:, s, :], acc[u, c][:], ACT.Sin, bias=half_slot[:, c : c + 1], scale=0.5)
+            return first
+
+        def turn_group(u, k, first):
+            side = PASS // widths[u]
+            road = ROADS[u][k]
+            if road == "scalar":
+                return first
+            second = new_tile([P, side, widths[u]], F32, "second%d%d" % (u, k), "neg_c", 4)
+            if road == "fold":
+                nc.vector.scalar_tensor_tensor(second[:], first[:], -1.0, first[:], ALU.mult, ALU.max)
+            else:
+                nc.vector.scalar_tensor_tensor(second[:], first[:], -2.0, first[:], ALU.mult, ALU.mult)
+            return second
+
+        def close_group(u, k, values):
             j0, j1 = CHUNKS[u]
             side = PASS // widths[u]
-            n_groups = T2 // P // side
-            for k in range(n_groups):
-                mid = new_tile([P, side, widths[u]], F32, "mid%d%d" % (u, k), "mid", 4)
-                result = new_tile([P, side, widths[u]], F32, "result%d%d" % (u, k), "result", 6)
-                road = ROADS[u][k]
-                spare = None if road == "scalar" else new_tile([P, side, widths[u]], F32, "spare%d%d" % (u, k), "spare", 2)
-                for s in range(side):
-                    c = k * side + s
-                    compare(1, u, c)
-                    if road == "scalar":
-                        nc.scalar.activation(mid[:, s, :], acc[u, c][:], ACT.Abs, bias=slot_t[:, c : c + 1])
-                    elif road == "fold":
-                        nc.vector.tensor_scalar(spare[:, s, :], acc[u, c][:], slot_t[:, c : c + 1], None, ALU.add)
-                    else:
-                        nc.scalar.activation(mid[:, s, :], acc[u, c][:], ACT.Sin, bias=half_slot[:, c : c + 1], scale=0.5)
-                if road == "square":
-                    nc.vector.scalar_tensor_tensor(spare[:], mid[:], -2.0, mid[:], ALU.mult, ALU.mult)
-                    nc.vector.tensor_scalar(result[:], spare[:], 1.0, None, ALU.add)
-                else:
-                    if road == "fold":
-                        nc.vector.scalar_tensor_tensor(mid[:], spare[:], -1.0, spare[:], ALU.mult, ALU.max)
-                    nc.scalar.activation(result[:], mid[:], ACT.Sin, bias=math.pi / 2, scale=-1.0)
-                rows = out[k * side * P : (k + 1) * side * P, j0:j1]
-                nc.sync.dma_start(rows.rearrange("(s p) j -> p s j", p=P), result[:])
+            result = new_tile([P, side, widths[u]], F32, "result%d%d" % (u, k))
+            if ROADS[u][k] == "square":
+                nc.vector.tensor_scalar(result[:], values[:], 1.0, None, ALU.add)
+            else:
+                nc.scalar.activation(result[:], values[:], ACT.Sin, bias=math.pi / 2, scale=-1.0)
+            rows = out[k * side * P : (k + 1) * side * P, j0:j1]
+            nc.sync.dma_start(rows.rearrange("(s p) j -> p s j", p=P), result[:])
 
         (j0, j1), (j1, j2) = CHUNKS
-        for c in range(T2 // P):
-            compare(0, 0, c)
-        x_bf1 = new_tile([P, PACK, j1 - j0], BF16, "x_bf10", "turn_y")
-        fetch(1, range(PACK), j0, j1, x_bf1, new_tile([P, PACK, j1 - j0], F32, "picked10", "turn_page"))
-        x_grouped1 = new_tile([P, j1 - j0, PACK], BF16, "x_grouped10", "turn_x")
-        weave(nc.scalar.copy, x_grouped1, x_bf1, X_VECTOR_COLS, j1 - j0)
-        page_q.append(quantize(page_bf1, T2, "page_q1"))
-        weave(nc.vector.tensor_copy, x_grouped1, x_bf1, 0, X_VECTOR_COLS)
-        quantize_into(x_q[1], slice(j0, j1), x_grouped1)
-        x_grouped0 = group_first_half(1, "turn_y")
-        read_out(0)
+        x_bf1 = new_tile([P, PACK, j1 - j0], BF16, "x_bf10")
+        picked = new_tile([P, PACK, j1 - j0], F32, "picked10", "raw")
+        pick(1, range(PACK), j0, j1, picked)
+        clamp(1, range(PACK), x_bf1, picked)
+        quantize_into(page_q[0], slice(0, T2), page_bf0)
+        x_grouped = new_tile([P, 2, j1 - j0, PACK], BF16, "x_grouped_first", "turn_x")
+        weave(nc.scalar.copy, x_grouped[:, 1], x_bf1, 0, P)
+        weave(nc.vector.tensor_copy, x_grouped[:, 1], x_bf1, P, 2 * P)
+        for c0 in range(0, j1 - j0, P):
+            weave(nc.scalar.copy, x_grouped[:, 0], x_joined[:, :, j0:j1], c0, c0 + P)
+        quantize_into(page_q[1], slice(0, T2), page_bf1)
+        quantize_into(x_q[1], slice(j0, j1), x_grouped[:, 1])
+        quantize_into(x_q[0], slice(j0, j1), x_grouped[:, 0])
+        x_grouped0 = new_tile([P, j2 - j1, PACK], BF16, "x_grouped01")
+        for c0 in range(0, j2 - j1, P):
+            weave(nc.scalar.copy, x_grouped0, x_joined[:, :, j1:j2], c0, c0 + P)
+        for k in range(3):
+            first = new_tile([P, 2, j1 - j0], F32, "first0%d" % k, "early%d" % (k % 2))
+            close_group(0, k, open_group(0, k, first[:]))
 
         x_bf1 = new_tile([P, PACK, j2 - j1], BF16, "x_bf11")
-        fetch(1, range(PACK), j1, j2, x_bf1, new_tile([P, PACK, j2 - j1], F32, "picked11", "turn_x"))
+        picked = new_tile([P, PACK, j2 - j1], F32, "picked11", "turn_x")
+        pick(1, range(PACK), j1, j2, picked)
+        clamp(1, range(PACK), x_bf1, picked)
         quantize_into(x_q[0], slice(j1, j2), x_grouped0)
-        for c in range(T2 // P):
+        for c in range(6):
             compare(0, 1, c)
-        x_grouped1 = new_tile([P, j2 - j1, PACK], BF16, "x_grouped11")
+        x_grouped1 = new_tile([P, j2 - j1, PACK], BF16, "x_grouped11", "turn_z")
         halves = [slice(c0, c0 + P) for c0 in range(0, j2 - j1, P)]
         for cols in halves:
             weave(nc.vector.tensor_copy, x_grouped1, x_bf1, cols.start, cols.stop)
         for cols in halves:
             quantize_into(x_q[1], slice(j1 + cols.start, j1 + cols.stop), x_grouped1[:, cols, :])
-        read_out(1)
+        last = open_group(0, 3, new_tile([P, 2, j1 - j0], F32, "first03", "turn_z")[:])
+        for c in range(6, 8):
+            compare(0, 1, c)
+        opened = [open_group(1, k, new_tile([P, 2, j2 - j1], F32, "first1%d" % k, "raw_small", 4)[:]) for k in range(3)]
+        last = turn_group(0, 3, last)
+        opened = [turn_group(1, k, opened[k]) for k in range(3)]
+        close_group(0, 3, last)
+        close_group(1, 0, opened[0])
+        opened.append(open_group(1, 3, new_tile([P, 2, j2 - j1], F32, "first13", "raw_small", 4)[:]))
+        for k in range(1, 4):
+            close_group(1, k, opened[k])

import math
from contextlib import ExitStack

import concourse.mybir as mybir
from concourse.masks import make_identity

K, T, S, H, T2, NX = 1024, 2048, 512, 1024, 1024, 512
FLOPS = 2 * K * H * S * 3 + 2 * H * T2 * NX

F32 = mybir.dt.float32
BF16 = mybir.dt.bfloat16
I32 = mybir.dt.int32
U32 = mybir.dt.uint32
U16 = mybir.dt.uint16
U8 = mybir.dt.uint8
FP8X4 = mybir.dt.float8_e4m3fn_x4
FP4X4 = mybir.dt.float4_e2m1fn_x4
ALU = mybir.AluOpType
ACT = mybir.ActivationFunctionType

P = 128
PACK = 4
PASS = P * PACK
W3_ROW = 4
CHUNKS = ((0, 256), (256, 512))
X_VECTOR_COLS = 64
FIRST_TAGS = (("early0", "early1", "early0", "early1"), ("h0_0", "early1", "early0", "h0_1"))
VW0_TAG = None
ROADS = (("scalar", "scalar", "scalar", "fold"), ("fold", "square", "square", "scalar"))


def weave(engine_copy, dst, src, c0, c1):
    engine_copy(
        out=dst[:, c0:c1, :].rearrange("p (c i) t -> p c t i", i=4),
        in_=src[:, :, c0:c1].rearrange("p t (c i) -> p c t i", i=4),
    )


def tile_list_mix_slot_readout_kernel(
    tc, tab_words, tab_scales, offs, offs2, offs3, w1, w2_words, w2_scales, w3_words, w3_scales,
    wgs, page0, low, look, slot, out,
):
    nc = tc.nc
    with ExitStack() as ctx:
        lists = ctx.enter_context(tc.tile_pool(name="lists", bufs=1))
        sb = ctx.enter_context(tc.tile_pool(name="sb", bufs=1))
        ps = ctx.enter_context(tc.psum_pool(name="ps", bufs=2))

        def new_tile(shape, dtype, name, tag=None, bufs=1):
            return sb.tile(shape, dtype, name=name, tag=tag or name, bufs=bufs, align_bytes=64)

        idx = lists.tile([P, S // 16], U16, name="idx")
        idx2 = lists.tile([P, S // 16], U16, name="idx2")
        idx3 = lists.tile([P, NX // 16], U16, name="idx3")

        n_ct = PASS // P
        n_jt = S // P
        tab_w = new_tile([P, 2, T], I32, "tab_w", tag="wide")
        tab_s = new_tile([P, 2, T], U8, "tab_s", tag="tab_s")
        w2_s = new_tile([P, 2, H], U8, "w2_s")
        w3_s = new_tile([P, 2, H], U8, "w3_s")
        warm = new_tile([P, 2], F32, "warm")
        wg_rows = new_tile([P, S], F32, "wg_rows")
        wg_dealt = new_tile([P, PACK, S], F32, "wg_dealt")
        r_parts = ((0, P), (P, 2 * P), (2 * P, PASS), (PASS, H))
        w2_w = [new_tile([P, 2, 2 * (r1 - r0)], U8, "w2_w%d" % r0) for r0, r1 in r_parts]
        w3_w = [new_tile([P, 2, r1 - r0], U32, "w3_w%d" % r0) for r0, r1 in r_parts]
        page = [[new_tile([P, T2], F32, "page%d%d" % (b, t)) for t in range(PACK)] for b in range(2)]
        low_t = [new_tile([P, PACK], F32, "low_t%d" % b) for b in range(2)]
        look_t = [new_tile([P, PACK], F32, "look_t%d" % b) for b in range(2)]
        slot_t = new_tile([P, T2 // P], F32, "slot_t")
        half_slot = new_tile([P, T2 // P], F32, "half_slot")
        ident = new_tile([P, P], F32, "ident")

        def load_table_words(a):
            nc.sync.dma_start(tab_w[:, a, :], tab_words[a].rearrange("p n i -> p (n i)").bitcast(I32))

        def load_scales(queue, plane, row0, scales):
            for q in (0, 2, 1, 3):
                queue.dma_start(
                    plane[32 * q + row0 : 32 * q + row0 + 4].bitcast(I32),
                    scales[:, 4 * q : 4 * q + 4, :].rearrange("a r n -> r a n").bitcast(I32),
                )

        def load_w1(a, r0, r1, tag, bufs):
            raw = new_tile([P, PACK, r1 - r0], F32, "w1_raw%d_%d" % (a, r0), tag, bufs)
            rows = w1[a * PASS : (a + 1) * PASS, r0:r1]
            nc.sync.dma_start(raw[:], rows.rearrange("(p i) c -> p i c", i=PACK))
            return raw

        def load_w2(part):
            r0, r1 = r_parts[part]
            nc.sync.dma_start(
                w2_w[part][:].bitcast(I32), w2_words[:, :, 2 * r0 : 2 * r1].rearrange("a p n -> p a n").bitcast(I32)
            )

        def load_w3(part):
            r0, r1 = r_parts[part]
            nc.sync.dma_start(
                w3_w[part][:].bitcast(I32), w3_words[:, :, r0:r1, :].rearrange("a p n i -> p a (n i)").bitcast(I32)
            )

        def load_page(b, t):
            rows = page0[b * PASS : (b + 1) * PASS, :]
            if b == 0:
                nc.sync.dma_start(page[b][t][:], rows[t * P : (t + 1) * P, :])
            else:
                nc.sync.dma_start(page[b][t][:], rows.rearrange("(p t) m -> p t m", t=PACK)[:, t, :])

        def mx_tiles(width, name, tag=None):
            return new_tile([P, width], U32, name + "_c", tag), new_tile([P, width], U8, name + "_s")

        def quantize_into(operand, cols, grouped):
            nc.vector.quantize_mx(
                out=operand[0][:, cols].bitcast(FP8X4), scales=operand[1][:, cols],
                in_=grouped[:].rearrange("p c t -> p (c t)"),
            )

        def quantize(grouped, width, name, tag=None):
            operand = mx_tiles(width, name, tag)
            quantize_into(operand, slice(0, width), grouped)
            return operand

        w1_q = [mx_tiles(H, "w1_q%d" % a) for a in range(2)]

        def group_w1(copy, raw, a, r0, r1, tag, bufs=1):
            grouped = new_tile([P, r1 - r0, PACK], BF16, "w1_bf%d_%d" % (a, r0), tag, bufs)
            for c0 in range(0, r1 - r0, P):
                weave(copy, grouped, raw, c0, c0 + P)
            return grouped

        nc.vector.memset(tab_s[:].bitcast(I32), 0)
        nc.gpsimd.memset(w2_s[:].bitcast(I32), 0)
        nc.vector.memset(w3_s[:].bitcast(I32), 0)
        nc.vector.memset(warm[:, 0:1], 0.0)
        nc.scalar.activation(warm[:, 1:2], warm[:, 0:1], ACT.Sin)
        nc.sync.dma_start(idx[:], offs)
        raw = {}
        raw[0, 0] = load_w1(0, 0, P, "raw_small", 4)
        load_w2(0)
        load_scales(nc.sync, tab_s, 0, tab_scales)
        load_table_words(0)
        load_table_words(1)
        load_scales(nc.sync, w2_s, 0, w2_scales)
        raw[1, 0] = load_w1(1, 0, P, "raw_small", 4)
        load_w3(0)
        load_scales(nc.sync, w3_s, W3_ROW, w3_scales)
        load_page(0, 0)
        nc.sync.dma_start(wg_rows[:, 0 : S // 2], wgs[:, 0 : S // 2])
        nc.sync.dma_start(idx2[:], offs2)
        make_identity(nc, ident[:])
        raw[0, 1] = load_w1(0, P, 2 * P, "raw_small", 4)
        raw[1, 1] = load_w1(1, P, 2 * P, "raw_small", 4)
        load_w2(1)
        nc.sync.dma_start(wg_rows[:, S // 2 : S], wgs[:, S // 2 : S])
        load_w3(1)
        raw[0, 2] = load_w1(0, 2 * P, PASS, "raw_mid", 2)
        nc.sync.dma_start(idx3[:], offs3)
        raw[1, 2] = load_w1(1, 2 * P, PASS, "raw_mid", 2)
        load_w2(2)
        load_w3(2)
        load_page(0, 1)
        raw01 = load_w1(0, PASS, H, "raw", 1)
        load_page(0, 2)
        raw11 = load_w1(1, PASS, H, "raw_b", 1)
        load_w2(3)
        load_w3(3)
        with nc.allow_non_contiguous_dma(reason="one value to a partition"):
            nc.sync.dma_start(low_t[0][:], low[0:PASS].rearrange("(c p) -> p c", p=P))
            nc.sync.dma_start(look_t[0][:], look[0:PASS].rearrange("(c p) -> p c", p=P))
        nc.sync.dma_start(low_t[1][:], low[PASS:H].rearrange("(p t) -> p t", t=PACK))
        nc.sync.dma_start(look_t[1][:], look[PASS:H].rearrange("(p t) -> p t", t=PACK))
        load_page(0, 3)
        for q in (0, 2, 1, 3):
            nc.sync.dma_start(wg_dealt[32 * q : 32 * q + 32], wgs.rearrange("(p t) j -> p t j", t=PACK))
        for t in range(PACK):
            load_page(1, t)
        with nc.allow_non_contiguous_dma(reason="one value of slot to a partition"):
            nc.sync.dma_start(slot_t[:], slot.rearrange("(c p) -> p c", p=P))
        nc.gpsimd.tensor_scalar(half_slot[:], slot_t[:], 0.5, 0.0, ALU.mult, ALU.add)

        v_s = [new_tile([P, S], U8, "v_s%d" % a) for a in range(2)]
        for a in range(2):
            nc.vector.tensor_copy(v_s[a][:], tab_s[:, a, :].indirect(idx[:]))
        v_w = [new_tile([P, S], U32, "v_w%d" % a, VW0_TAG if a == 0 else None) for a in range(2)]
        nc.vector.tensor_copy(v_w[0][:], tab_w[:, 0, :].bitcast(U32).indirect(idx[:]))
        for a in range(2):
            quantize_into(w1_q[a], slice(0, P), group_w1(nc.vector.tensor_copy, raw[a, 0], a, 0, P, "bf_small", 2))
        nc.vector.tensor_copy(v_w[1][:], tab_w[:, 1, :].bitcast(U32).indirect(idx[:]))

        def weights(c):
            cols = slice(c * P, (c + 1) * P)
            part, c0 = min(c, 2), max(c - 2, 0) * P
            return (
                [(w2_w[part][:, a, 2 * c0 : 2 * (c0 + P)].bitcast(FP4X4), w2_s[:, a, cols]) for a in range(2)],
                [(w3_w[part][:, a, c0 : c0 + P].bitcast(FP8X4), w3_s[W3_ROW:P, a, cols]) for a in range(2)],
                [(w1_q[a][0][:, cols].bitcast(FP8X4), w1_q[a][1][:, cols]) for a in range(2)],
            )

        def three_banks(shape, n):
            return (
                ps.tile(shape, F32, name="bank_b", tag="B%d" % (n % 2), bufs=1),
                ps.tile(shape, F32, name="bank_c", tag="C%d" % (n % 2), bufs=1),
                ps.tile(shape, F32, name="bank_a", tag="A"),
            )

        def put(b, t, h_part, j0, j1):
            offsets = idx2[:] if j1 - j0 == S else idx2[:, j0 // 16 : j1 // 16]
            gains = wg_rows[:, j0:j1] if b == 0 else wg_dealt[:, t, j0:j1]
            nc.vector.tensor_tensor(page[b][t][:].indirect(offsets), h_part, gains, ALU.mult)

        def direct(c, parts):
            banks = three_banks([P, S], c)
            bank_b, bank_c, bank_a = banks
            w_b, w_c, w_a = weights(c)
            order = (1, 0) if c else (0, 1)
            for bank, passes in ((bank_b, w_b), (bank_a, w_a), (bank_c, w_c)):
                for a in order:
                    nc.tensor.matmul_mx(
                        out=bank[:], lhsT=passes[a][0], lhsT_scale=passes[a][1],
                        rhs=v_w[a][:].bitcast(FP8X4), rhs_scale=v_s[a][:], start=(a == order[0]), stop=(a == order[1]),
                    )
            abs_b = new_tile([P, S], F32, "abs_b0%d" % c, "neg_c", 4)
            prod = new_tile([P, S], F32, "prod0%d" % c, "early%d" % (c % 2))
            h = new_tile([P, S], F32, "h0%d" % c, "h0_%d" % (c % 2))
            for j0, j1 in parts:
                nc.scalar.activation(abs_b[:, j0:j1], bank_b[:, j0:j1], ACT.Abs)
            for j0, j1 in parts:
                nc.vector.tensor_tensor(prod[:, j0:j1], bank_a[:, j0:j1], abs_b[:, j0:j1], ALU.mult)
            for j0, j1 in parts:
                nc.vector.tensor_tensor(h[:, j0:j1], prod[:, j0:j1], bank_c[:, j0:j1], ALU.subtract)
            return h

        def turn(neg_c, prod, tag):
            bank_h = ps.tile([P, PACK, P], F32, name="bank_h", tag=tag)
            for t in range(PACK):
                nc.tensor.matmul(bank_h[:, t, :], neg_c[:, t, :], ident[:], start=True, stop=False, is_transpose=True)
                nc.tensor.matmul(bank_h[:, t, :], prod[:, t, :], ident[:], start=False, stop=True, is_transpose=True)
            return bank_h

        def dealt(bank):
            return bank[:].rearrange("j (p t) -> j t p", t=PACK)

        def term(name, tag, bufs=1):
            return new_tile([P, PACK, P], F32, name, tag, bufs)[:]

        def products(jt, abs_b, neg_c, prod):
            cols = slice(jt * P, (jt + 1) * P)
            r_cols = slice(PASS, H)
            bank_b, bank_c, bank_a = three_banks([P, PASS], jt)
            moving = (
                (bank_b, [(w2_w[3][:, a, :].bitcast(FP4X4), w2_s[:, a, r_cols]) for a in range(2)]),
                (bank_c, [(w3_w[3][:, a, :].bitcast(FP8X4), w3_s[W3_ROW:P, a, r_cols]) for a in range(2)]),
                (bank_a, [(w1_q[a][0][:, r_cols].bitcast(FP8X4), w1_q[a][1][:, r_cols]) for a in range(2)]),
            )
            for bank, passes in moving:
                for a in (1, 0):
                    codes, scales = passes[a]
                    nc.tensor.matmul_mx(
                        out=bank[:], lhsT=v_w[a][:, cols].bitcast(FP8X4), lhsT_scale=v_s[a][:, cols],
                        rhs=codes, rhs_scale=scales, start=(a == 1), stop=(a == 0),
                    )
            nc.scalar.activation(abs_b, dealt(bank_b), ACT.Abs)
            nc.scalar.activation(neg_c, dealt(bank_c), ACT.Copy, scale=-1.0)
            nc.vector.tensor_tensor(prod, dealt(bank_a), abs_b, ALU.mult)
            return neg_c, prod

        def pick(b, ts, j0, j1, picked):
            offsets = idx3[:] if j1 - j0 == NX else idx3[:, j0 // 16 : j1 // 16]
            for n, t in enumerate(ts):
                nc.vector.tensor_copy(picked[:, n, :], page[b][t][:].indirect(offsets))

        def clamp(b, ts, x_bf, picked):
            for n, t in enumerate(ts):
                nc.vector.tensor_scalar(
                    x_bf[:, t, :], picked[:, n, :], low_t[b][:, t : t + 1], look_t[b][:, t : t + 1], ALU.max, ALU.mult
                )

        page_across = new_tile([P, T2 // P, 2, P, 2], BF16, "page_across", "wide")
        x_bf0 = new_tile([P, PACK, NX], BF16, "x_bf0")

        def page_rows_across(c, tags=(("H", 2), ("H", 2))):
            for m0, (tag, bufs) in zip(range(0, T2 // P, PACK), tags):
                bank = ps.tile([P, PACK, P], F32, name="bank_t", tag=tag, bufs=bufs)
                for i in range(PACK):
                    nc.tensor.transpose(bank[:, i, :], page[0][c][:, (m0 + i) * P : (m0 + i + 1) * P], ident[:])
                nc.scalar.copy(
                    out=page_across[:, m0 : m0 + PACK, :, 32 * c : 32 * c + 32, :],
                    in_=bank[:].rearrange("m i (p h e) -> m i h p e", h=2, e=2),
                )

        def back_down(across, i0, grouped, tag, bufs):
            words = across[:].rearrange("m i h p e -> m i h (p e)").bitcast(F32)
            bank = ps.tile([P, 2, 2, P], F32, name="bank_w", tag=tag, bufs=bufs)
            for i in range(2):
                for h in range(2):
                    nc.tensor.transpose(bank[:, i, h, :], words[:, i0 + i, h, :], ident[:])
            nc.scalar.copy(
                out=grouped.rearrange("p (i m) t -> p i (m t)", i=2).bitcast(F32).rearrange("p i (m h) -> p i m h", h=2),
                in_=bank[:].rearrange("p i h m -> p i m h"),
            )

        halves = ((0, S // 2), (S // 2, S))
        h_first = direct(0, halves)
        put(0, 0, h_first[:, 0 : S // 2], *halves[0])
        for a in range(2):
            quantize_into(w1_q[a], slice(P, 2 * P), group_w1(nc.scalar.copy, raw[a, 1], a, P, 2 * P, "bf1%d" % a))
        put(0, 0, h_first[:, S // 2 : S], *halves[1])
        h_second = direct(1, halves)
        picked = [new_tile([P, 1, NX], F32, "picked00")]
        pick(0, (0,), 0, NX, picked[0])
        for a in range(2):
            quantize_into(w1_q[a], slice(2 * P, PASS), group_w1(nc.scalar.copy, raw[a, 2], a, 2 * P, PASS, "bf2%d" % a))
        put(0, 1, h_second[:], 0, S)
        h_third = direct(2, halves)
        h_fourth = direct(3, halves)
        late = [group_w1(nc.scalar.copy, raw_late, a, PASS, H, "bf_late%d" % a) for a, raw_late in enumerate((raw01, raw11))]
        page_rows_across(0, (("B0", 1), ("B1", 1)))
        put(0, 2, h_third[:], 0, S)
        page_rows_across(1, (("C0", 1), ("C1", 1)))
        for a in range(2):
            quantize_into(w1_q[a], slice(PASS, H), late[a])
        clamp(0, (0,), x_bf0, picked[0])
        put(0, 3, h_fourth[:], 0, S)

        widths = [j1 - j0 for j0, j1 in CHUNKS]
        h1 = new_tile([P, PACK, S], F32, "h1", "raw")
        held = new_tile([P, 2, PACK, P], F32, "prod1_held", "wg_rows")
        prods = [held[:, 0], held[:, 1], term("prod12", "early0"), term("prod13", "early1")]

        def second_half_terms(jt):
            abs_b = term("abs_b1%d" % jt, "turn%d" % jt)
            return products(jt, abs_b, term("neg_c1%d" % jt, "neg_c", 4), prods[jt])

        terms = [second_half_terms(jt) for jt in range(n_jt)]
        page_rows_across(2, (("B0", 1), ("C0", 1)))
        for jt in range(n_jt):
            nc.scalar.copy(out=h1[:, :, jt * P : (jt + 1) * P], in_=turn(*terms[jt], "H" if jt < 2 else "A")[:])
        page_rows_across(3, (("B1", 1), ("C1", 1)))
        picked = [new_tile([P, 1, NX], F32, "picked01", "turn1"), new_tile([P, 2, NX], F32, "picked02", "turn3")]
        pick(0, (1,), 0, NX, picked[0])
        pick(0, (2, 3), 0, NX, picked[1])
        clamp(0, (1,), x_bf0, picked[0])
        clamp(0, (2, 3), x_bf0, picked[1])
        page_bf0 = new_tile([P, T2, PACK], BF16, "page_bf0", tag="turn_page")
        for n, tag in enumerate(("B0", "C0", "B1", "C1")):
            back_down(page_across, 2 * n, page_bf0[:, 2 * n * P : 2 * (n + 1) * P, :], tag, 1)
        x_joined = new_tile([P, PACK, NX], BF16, "x_joined")
        for c in (0, 2, 1, 3):
            for t in range(PACK):
                nc.sync.dma_start(x_joined[32 * c : 32 * c + 32, t, :], x_bf0[t:P:PACK, c, :])

        codes0 = new_tile([P, T2 + NX], U32, "codes0", "wg_dealt")
        x_q = [(codes0[:, T2 : T2 + NX], new_tile([P, NX], U8, "x_q0_s")), mx_tiles(NX, "x_q1")]
        page_q = [(codes0[:, 0:T2], new_tile([P, T2], U8, "page_q0_s")), mx_tiles(T2, "page_q1")]

        page_bf1 = new_tile([P, T2, PACK], BF16, "page_bf1", "wide")
        for t in range(PACK):
            put(1, t, h1[:, t, :], 0, S)
            nc.scalar.copy(out=page_bf1[:, :, t], in_=page[1][t][:])

        bank_slots = [("B0", 1), ("C0", 1), ("B1", 1), ("C1", 1), ("A", 2), ("A", 2), ("H", 2), ("H", 2)]

        acc = {}

        def compare(b, u, c):
            first = b == 0
            if first:
                acc[u, c] = ps.tile([P, widths[u]], F32, name="acc", tag=bank_slots[c][0], bufs=bank_slots[c][1])
            cols = slice(c * P, (c + 1) * P)
            picks = slice(*CHUNKS[u])
            nc.tensor.matmul_mx(
                out=acc[u, c][:], lhsT=page_q[b][0][:, cols].bitcast(FP8X4), lhsT_scale=page_q[b][1][:, cols],
                rhs=x_q[b][0][:, picks].bitcast(FP8X4), rhs_scale=x_q[b][1][:, picks], start=first, stop=not first,
            )

        def open_group(u, k, first):
            side = PASS // widths[u]
            road = ROADS[u][k]
            for s in range(side):
                c = k * side + s
                if u == 0:
                    compare(0, u, c)
                compare(1, u, c)
                if road == "scalar":
                    nc.scalar.activation(first[:, s, :], acc[u, c][:], ACT.Abs, bias=slot_t[:, c : c + 1])
                elif road == "fold":
                    nc.vector.tensor_scalar(first[:, s, :], acc[u, c][:], slot_t[:, c : c + 1], None, ALU.add)
                else:
                    nc.scalar.activation(first[:, s, :], acc[u, c][:], ACT.Sin, bias=half_slot[:, c : c + 1], scale=0.5)
            return first

        def turn_group(u, k, first):
            side = PASS // widths[u]
            road = ROADS[u][k]
            if road == "scalar":
                return first
            second = new_tile([P, side, widths[u]], F32, "second%d%d" % (u, k), "neg_c", 4)
            if road == "fold":
                nc.vector.scalar_tensor_tensor(second[:], first[:], -1.0, first[:], ALU.mult, ALU.max)
            else:
                nc.vector.scalar_tensor_tensor(second[:], first[:], -2.0, first[:], ALU.mult, ALU.mult)
            return second

        def close_group(u, k, values):
            j0, j1 = CHUNKS[u]
            side = PASS // widths[u]
            result = new_tile([P, side, widths[u]], F32, "result%d%d" % (u, k))
            if ROADS[u][k] == "square":
                nc.vector.tensor_scalar(result[:], values[:], 1.0, None, ALU.add)
            else:
                nc.scalar.activation(result[:], values[:], ACT.Sin, bias=math.pi / 2, scale=-1.0)
            rows = out[k * side * P : (k + 1) * side * P, j0:j1]
            nc.sync.dma_start(rows.rearrange("(s p) j -> p s j", p=P), result[:])

        (j0, j1), (j1, j2) = CHUNKS
        x_bf1 = new_tile([P, PACK, j1 - j0], BF16, "x_bf10")
        picked = new_tile([P, PACK, j1 - j0], F32, "picked10", "raw")
        pick(1, range(PACK), j0, j1, picked)
        clamp(1, range(PACK), x_bf1, picked)
        quantize_into(page_q[0], slice(0, T2), page_bf0)
        x_grouped = new_tile([P, 2, j1 - j0, PACK], BF16, "x_grouped_first", "turn_x")
        weave(nc.scalar.copy, x_grouped[:, 1], x_bf1, 0, P)
        weave(nc.vector.tensor_copy, x_grouped[:, 1], x_bf1, P, 2 * P)
        for c0 in range(0, j1 - j0, P):
            weave(nc.scalar.copy, x_grouped[:, 0], x_joined[:, :, j0:j1], c0, c0 + P)
        quantize_into(page_q[1], slice(0, T2), page_bf1)
        quantize_into(x_q[1], slice(j0, j1), x_grouped[:, 1])
        quantize_into(x_q[0], slice(j0, j1), x_grouped[:, 0])
        x_grouped0 = new_tile([P, j2 - j1, PACK], BF16, "x_grouped01")
        for c0 in range(0, j2 - j1, P):
            weave(nc.scalar.copy, x_grouped0, x_joined[:, :, j1:j2], c0, c0 + P)
        for k in range(3):
            first = new_tile([P, 2, j1 - j0], F32, "first0%d" % k, "early%d" % (k % 2))
            close_group(0, k, open_group(0, k, first[:]))

        x_bf1 = new_tile([P, PACK, j2 - j1], BF16, "x_bf11")
        picked = new_tile([P, PACK, j2 - j1], F32, "picked11", "turn_x")
        pick(1, range(PACK), j1, j2, picked)
        clamp(1, range(PACK), x_bf1, picked)
        quantize_into(x_q[0], slice(j1, j2), x_grouped0)
        for c in range(6):
            compare(0, 1, c)
        x_grouped1 = new_tile([P, j2 - j1, PACK], BF16, "x_grouped11", "turn_z")
        halves = [slice(c0, c0 + P) for c0 in range(0, j2 - j1, P)]
        for cols in halves:
            weave(nc.vector.tensor_copy, x_grouped1, x_bf1, cols.start, cols.stop)
        for cols in halves:
            quantize_into(x_q[1], slice(j1 + cols.start, j1 + cols.stop), x_grouped1[:, cols, :])
        last = open_group(0, 3, new_tile([P, 2, j1 - j0], F32, "first03", "turn_z")[:])
        for c in range(6, 8):
            compare(0, 1, c)
        opened = [open_group(1, k, new_tile([P, 2, j2 - j1], F32, "first1%d" % k, "raw_small", 4)[:]) for k in range(3)]
        last = turn_group(0, 3, last)
        opened = [turn_group(1, k, opened[k]) for k in range(3)]
        close_group(0, 3, last)
        close_group(1, 0, opened[0])
        opened.append(open_group(1, 3, new_tile([P, 2, j2 - j1], F32, "first13", "raw_small", 4)[:]))
        for k in range(1, 4):
            close_group(1, k, opened[k])
